import numpy as np, ml_dtypes
CORES = [35,38,43,46]
N = 4
BF = ml_dtypes.bfloat16
V, M, W, TR, RO, CAP = 512, 256, 4096, 4, 3, 60
def spot(a, b, p, q):
    return ((a * (2 * b + 1) >> 4) + a + p * (2 * b + 613) + q * (2 * a + 37)) & (W - 1)
def look(X, a, b, p, q):
    return np.take_along_axis(X, spot(a, b, p, q).reshape(N, 8, 1, 16 * M), 3).reshape(N, 8, 16, 16, M)
def excess(R, z):
    return np.add.reduce(np.maximum(R - z[:, :, :, None, :], 0), axis=2)
def scan(X, G, B, d, z, t):
    ra = np.arange(N)[:, None, None, None]; ga = np.arange(8)[None, :, None, None]; z = z.astype(np.int32)
    n = np.add.reduce((G >= 0).astype(np.int64), axis=2)
    s = np.where((G >= 0) & ((G & 1) == (t & 1)), n[ra, ga, np.maximum(G, 0)], -1)
    e = np.take_along_axis(G, np.argmax(s, axis=2)[:, :, None, :], 2)[:, :, 0]
    e = np.where(np.max(s, axis=2) >= 0, e, -1)
    v = 2 * np.arange(M) + (t & 1); L = G[..., v]; on = L >= 0; a = np.maximum(L, 0)
    old = d[ra, ga, a]; mine = on & (e[ra, ga, a] == v); dv = d[:, :, v][:, :, None, :]
    new = old; pick = look(X, a, v, old, dv); low = excess(pick, z)
    for j in range(1, TR):
        p = (old + j) & 15; R = look(X, a, v, p, dv); x = excess(R, z); w = mine & (x < low)
        low = np.where(w, x, low); new = np.where(w, p, new); pick = np.where(w[:, :, None], R, pick)
    up = np.max(np.where(on[:, :, None], pick, 0), axis=3)
    o = np.take_along_axis(B, a, 3); both = np.concatenate([d, np.roll(d, -1, axis=0)], axis=2); do = both[ra, ga, o]
    dmg = np.where(on, excess(look(X, o, a, do, new), z) - excess(look(X, o, a, do, old), z), -99999)
    k = np.argmax(dmg, axis=2)[:, :, None, :]
    return n[:, :, v], v, L, a, mine, new, up, np.take_along_axis(dmg, k, 2)[:, :, 0], np.take_along_axis(o, k, 2)[:, :, 0]
def graph(rng, S, share):
    m = np.argsort(rng.random((S, V)), axis=1); i = np.arange(S)[:, None]; mate = np.zeros((S, V), np.int64)
    mate[i, m[:, :M]] = m[:, M:]; mate[i, m[:, M:]] = m[:, :M]
    act = 0.3 + 0.7 * rng.random(V); act[rng.random(V) < 0.04] = 0.0
    r = rng.random((S, V))[i, np.minimum(mate, np.arange(V))]
    return np.where(r < share * act * act[mate], mate, -1)
def tidy(tab):
    tab = np.array(tab, np.int64)
    for k in range(1, len(tab)): tab[k] = np.where(np.any(tab[:k] == tab[k], axis=0), -1, tab[k])
    tab = np.take_along_axis(tab, np.argsort(tab < 0, axis=0, kind="stable"), 0)[:16]
    return np.concatenate([tab, np.full((16 - len(tab), V), -1, np.int64)])
def plain(rng, share):
    return tidy(np.concatenate([np.where(rng.random((1, V)) < 0.15, np.arange(V), -1), graph(rng, 16, share)]))
def blocks(rng, own):
    p = rng.permutation(V).reshape(-1, 16); tab = np.zeros((16, V), np.int64)
    o = np.argsort(rng.random((len(p), 16, 16)), axis=2)
    tab[:, p.reshape(-1)] = p[np.arange(len(p))[:, None, None], o].reshape(-1, 16).T
    return tab if own else tidy(np.where(tab == np.arange(V), -1, tab))
def edges():
    return np.concatenate([np.arange(8), np.arange(V - 8, V)])
def corner(rng):
    c = edges(); tab = c[np.argsort(rng.random((16, V)), axis=0)]
    size = rng.choice(np.array([16, 16, 15, 14, 2, 0]), V); size[c] = rng.choice(np.array([16, 16, 15, 14]), 16)
    tab[:2, size == 2] = np.array([[0], [V - 1]])
    for u in (0, V - 1): tab[:, u] = np.concatenate([[V - 2], rng.permutation(c[c != V - 2])])
    tab[:, V - 2] = np.concatenate([[0], rng.permutation(c[1:15]), [V - 1]]); size[[0, V - 2, V - 1]] = 16
    return np.where(np.arange(16)[:, None] < size, tab, -1)
def lift(rng, rec, z, a, v, dv, o, do):
    def ex(x): return np.add.reduce(np.maximum(rec[:, x] - z.reshape((16,) + (1,) * (x.ndim - 1) + (-1,)), 0), axis=0)
    p = np.arange(16)[:, None]; E = ex(spot(a, v, p, dv))
    new = (p + np.argmin(np.stack([np.roll(E, -j, axis=0) for j in range(TR)]), axis=0)) & 15
    F = ex(spot(o[:, None], a, do[:, None], p))
    D = np.take_along_axis(F, np.broadcast_to(new, F.shape), 1) - F
    s = np.where(D > 0, 1 + rng.random(D.shape) + 2 * (np.arange(len(o))[:, None, None] == 0), 0)
    b = np.argmax(s.reshape(-1, s.shape[-1]), axis=0)
    return b & 15, b >> 4
def parts(rng):
    gl = np.stack([np.stack([plain(rng, float(rng.choice(np.array([0.7, 1.0, 1.5, 2.5])))) for g in range(8)]) for r in range(N)])
    rec = (256 * rng.random((N, 8, 16, W)) * (0.4 + 0.6 * rng.random((N, 8, 1, W)))).astype(np.int64)
    val = rng.integers(0, 16, (N, 8, V)); zl = (256 * rng.random((N, 8, 16, M)) ** 1.5).astype(np.int64)
    th = (rng.choice(np.array([4, 40, 200, 1000]), (N, 8, M)) * rng.random((N, 8, M))).astype(np.int64)
    gs = rng.choice(np.array([0.3, 0.5, 0.8]), (N, 8, 1, 1)); full = rng.integers(0, 8, N); gs[np.arange(N), full] = 1.0; th[np.arange(N), full] = rng.integers(0, 8, (N, M))
    nb = rng.integers(0, V, (N, 8, 16, V)) + V * (rng.random((N, 8, 16, V)) < gs)
    return rec, gl, nb, val, zl, th
def pack(rec, gl, nb, val, zl, th):
    return {"rec": rec.reshape(N, 128, W).astype(np.float32).astype(BF), "gl": np.ascontiguousarray(gl.reshape(N, 128, V)).astype(np.int32), "nb": np.ascontiguousarray(nb.reshape(N, 128, V)).astype(np.int32),
            "val": val.astype(np.int32), "zl": zl.reshape(N, 128, M).astype(np.float32).astype(BF), "th": th.astype(np.int32)}
def largest(rec, gl, nb, val, zl):
    return scan(rec.astype(np.int32), gl, nb, val, zl, 0)[7]
def tune(rng, top, want):
    pos = np.argsort(np.argsort(np.where(top > 0, rng.random(top.shape), 2.0), axis=2), axis=2); sel = (pos < want) & (top > 0); coin = rng.random(top.shape)
    low = np.where(coin < 0.5, top - 1, (rng.random(top.shape) * top).astype(np.int64))
    return np.where(sel, low, np.where(coin < 0.1, 4080, np.maximum(top, 0)))
def setup_inputs(rng):
    return pack(*parts(rng))
def setup_inputs_spread(rng):
    rec, gl, nb, val, zl, th = parts(rng)
    rec = (np.exp2(8 * rng.random((N, 8, 1, W))) * rng.random((N, 8, 16, W))).astype(np.int64)
    zl = (np.exp2(8 * rng.random((N, 8, 1, M))) * rng.random((N, 8, 16, M))).astype(np.int64)
    th = np.minimum((np.exp2(12 * rng.random((N, 8, M)) ** 1.5) - 1).astype(np.int64), 4080)
    nb = (2 * V * rng.random((N, 8, 16, V)) ** 1.5).astype(np.int64); val = (16 * rng.random((N, 8, V)) ** 2).astype(np.int64)
    return pack(rec, gl, nb, val, zl, th)
def setup_inputs_ends(rng):
    rec, gl, nb, val, zl, th = parts(rng)
    rec = 255 * np.where(rng.random((N, 8, 1, W)) < 0.8, rng.integers(0, 2, (N, 8, 1, W)), rng.integers(0, 2, (N, 8, 16, W)))
    val = 15 * rng.integers(0, 2, (N, 8, V)); th = 4080 * (rng.random((N, 8, M)) < 0.4).astype(np.int64)
    zl = 255 * np.where(rng.random((N, 8, 1, M)) < 0.6, rng.random((N, 8, 1, M)) < 0.35, rng.random((N, 8, 16, M)) < 0.35).astype(np.int64)
    e = rng.random((N, 8, 16, V)); nb = np.where(e < 0.4, 0, np.where(e < 0.85, 2 * V - 1, nb))
    for r in range(N):
        few = [6, 7] + [int(g) for g in rng.permutation(6)[:2]]
        for g in range(8):
            gl[r, g] = corner(rng) if g in few else tidy(np.concatenate([graph(rng, 14, 1.5), np.zeros((1, V), np.int64), np.full((1, V), V - 1, np.int64)]))
    for g in (6, 7):
        val[:, g, 0] = 15; val[:, g, V - 2] = 0; val[:, g, V - 1] = 0; zl[:, g, :, M - 1] = 0
        th[:, g, M - 1] = np.where(np.arange(N) % 2 == 1, 0, 4080)
        nb[:, g, 15, V - 1] = 2 * V - 1; nb[:, g, 0, 0] = 0 if g == 7 else 2 * V - 1
        hi = [spot(0, V - 2, 15, 0), spot(V - 1, V - 2, 0, 0), spot(2 * V - 1, V - 1, 0, 1), spot(0, 0, 15, 0) if g == 7 else spot(2 * V - 1, 0, 0, 15)]
        lo = [spot(0, V - 2, 0, 0), spot(V - 1, V - 2, 1, 0), spot(2 * V - 1, V - 1, 0, 0), spot(0, 0, 15, 15) if g == 7 else spot(2 * V - 1, 0, 0, 0)]
        for x in lo: rec[:, g, :, x] = 0
        for x in hi: rec[:, g, :, x] = 255
    return pack(rec, gl, nb, val, zl, th)
def setup_inputs_corners(rng):
    rec, gl, nb, val, zl, th = parts(rng); c = edges(); late = []
    for r in range(N):
        for g, k in enumerate(rng.permutation(8)):
            if k == 0:
                ev = np.concatenate([[V - 2], 2 * rng.permutation(M - 1)]); od = 2 * rng.permutation(M) + 1; h = M // 2
                tab = np.full((16, V), -1, np.int64)
                tab[0, ev[:h]] = od[:h]; tab[0, od[:h]] = ev[:h]; tab[0, od[h:]] = ev[:h]; tab[1, od[h:]] = ev[h:]; tab[0, ev[h:]] = od[h:]
                late.append((r, g, ev[:h], od[:h], od[h:]))
            elif k == 1: tab = blocks(rng, True)
            elif k == 2: tab = blocks(rng, False)
            elif k == 3:
                tab = graph(rng, 16, 2.0); tab = tidy(np.where((tab & 1 == 1) & (np.arange(V) & 1 == 1), tab, -1))
            elif k == 4:
                tab = graph(rng, 16, 2.0); off = rng.random(V) < 0.5; tab = tidy(np.where(off | off[tab], -1, tab))
            elif k == 5:
                tab = np.argsort(rng.random((V, V)), axis=1)[:, :16].T; tab = np.where(np.arange(16)[:, None] < rng.integers(0, 17, V), tab, -1)
            elif k == 6:
                tab = c[np.argsort(rng.random((16, V)), axis=0)]; tab[:, c] = np.argsort(rng.random((16, V)), axis=1)[:, :16].T
            else: tab = plain(rng, 1.5)
            gl[r, g] = tab
    m = np.arange(V); e = rng.integers(0, 10, (N, 8, 16, V))
    for k, x in enumerate((0, V - 1, V, 2 * V - 1, m, m + V)): nb = np.where(e == k, x, nb)
    e = rng.integers(0, 4, (N, 8, V)); val = np.where(e == 0, 0, np.where(e == 1, 15, val))
    e = rng.integers(0, 6, (N, 8, 1, M)); zl = np.where(e == 0, 0, np.where(e == 1, 255, zl >> 1))
    want = rng.choice(np.array([0, 1, CAP - 1, CAP, CAP + 1, M]), (N, 8, 1))
    for r, g, v, a, o in late:
        zl[r, g, :, M - 1] = 0; dv = val[r, g, v]; do = val[r, g, o]; q = (np.arange(16) + 1) & 15
        x = spot(a[0], v[0], np.arange(16), dv[0]); y = spot(o[0], a[0], do[0], np.arange(16))
        s = int(np.argmax((x != y) & (x[q] != y[q]))); u = int(q[s])
        rec[r, g, :, int(x[s])] = 255; rec[r, g, :, int(y[u])] = 255; rec[r, g, :, int(x[u])] = 0; rec[r, g, :, int(y[s])] = 0
        p = lift(rng, rec[r, g], zl[r, g][:, v >> 1], a, v, dv, o[None], do[None])[0]
        val[r, g, a] = p; val[r, g, a[0]] = s; nb[r, g][:, a] = o; want[r, g, 0] = M
    th = tune(rng, largest(rec, gl, nb, val, zl), want)
    for r, g, v, a, o in late: th[r, g, M - 1] = 4079
    return pack(rec, gl, nb, val, zl, th)
def setup_inputs_crowd(rng):
    rec, gl, nb, val, zl, th = parts(rng); zl = zl >> 1; ev = 2 * np.arange(M)
    spots = np.array([V, 2 * V - 1, V + M]); cnt = np.array([CAP, CAP + 1, CAP - 1, M, CAP + 1]); want = np.zeros((N, 8, 1), np.int64)
    for r in range(N):
        most = ((2, 3), (4, 5), (3, 2), (5, 4))[r % 4]
        left = [g for g in range(1, 8) if g not in most]
        want[r, left, 0] = cnt if r == 0 else rng.permutation(cnt)
        want[r, most[0], 0] = M; want[r, most[1], 0] = M - 1
        for g in range(8):
            gl[r, g] = plain(rng, 1.5); s = int(rng.choice(spots))
            if g in most:
                od = 2 * rng.permutation(M) + 1; tab = np.full((16, V), -1, np.int64); tab[0, ev] = od; tab[0, od] = ev; gl[r, g] = tab
                o = np.tile(rng.permutation(spots)[:, None], (1, M))
                p, k = lift(rng, rec[r, g], zl[r, g], od, ev, val[r, g, ev], o, val[(r + 1) % N, g][o - V])
                val[r, g, od] = p; nb[r, g] = o[0, 0]; nb[r, g][:, od] = o[k, np.arange(M)]
            elif g == 0: nb[r, g] = (0, V - 1)[r % 2]
            elif g < 5: nb[r, g] = s
            elif g == 5: nb[r, g] = rng.choice(spots, (16, V))
            else: nb[r, g] = np.where(rng.random((16, V)) * CAP < 1, 2 * V - 1 if s == V else V, s)
    top = largest(rec, gl, nb, val, zl); got = np.minimum(np.add.reduce((top > 0).astype(np.int64), axis=2), want[:, :, 0])
    for r in range(N): want[r, 0, 0] = ((31, 0)[r % 2] - int(np.add.reduce(got[r, 1:]))) & 31
    return pack(rec, gl, nb, val, zl, tune(rng, top, want))
def check_inputs(d):
    bad = []
    for k, lo, hi in (("rec", 0, 255), ("gl", -1, V - 1), ("nb", 0, 2 * V - 1), ("val", 0, 15), ("zl", 0, 255), ("th", 0, 4080)):
        x = np.asarray(d[k]).astype(np.float64)
        if not (np.min(x) >= lo and np.max(x) <= hi): bad.append("range of " + k)
        if np.any(x != np.floor(x)): bad.append("whole numbers in " + k)
    g = np.asarray(d["gl"]).reshape(N, 8, 16, V); on = g >= 0; s = np.sort(g, axis=2)
    if np.any(on[:, :, 1:] & ~on[:, :, :-1]): bad.append("gl: a name after an empty slot")
    if np.any((s[:, :, 1:] == s[:, :, :-1]) & (s[:, :, 1:] >= 0)): bad.append("gl: a name twice in one list")
    return bad
def reference(rec, gl, nb, val, zl, th):
    X = rec.astype(np.float32).astype(np.int32).reshape(N, 8, 16, W); G = gl.astype(np.int64).reshape(N, 8, 16, V); B = nb.astype(np.int64).reshape(N, 8, 16, V)
    d = val.astype(np.int64); z = zl.astype(np.float32).astype(np.int32).reshape(N, 8, 16, M); h = th.astype(np.int64); c = np.zeros((N, 1, 1), np.int64)
    for t in range(RO):
        n, v, L, a, mine, new, up, top, who = scan(X, G, B, d, z, t)
        hurt = top > h + (c & 31)
        c = np.add.reduce(hurt.astype(np.int64).reshape(N, 8 * M), axis=1).reshape(N, 1, 1)
        z = np.roll((z + up) >> 1, 1 + t, axis=0)
        w = np.nonzero(mine); d = d + 0; d[w[0], w[1], a[w]] = new[w]
        gh = (hurt & (who >= V)).astype(np.int64); told = (gh == 1) & (np.add.accumulate(gh, axis=2) - gh < CAP)
        w = np.nonzero(told); np.add.at(d, ((w[0] + 1) % N, w[1], who[w] - V), 1); d = d & 15
        w = np.nonzero(hurt & (who < V) & (n < 16) & ~np.any(L == who[:, :, None, :], axis=2))
        G[w[0], w[1], n[w], v[w[2]]] = who[w]
    return {"yl": G.reshape(N, 128, V).astype(np.float32), "yd": d.astype(np.float32), "yz": z.reshape(N, 128, M).astype(np.float32).astype(BF)}

@@ -1,0 +1,712 @@
+from concourse.mybir import AluOpType, ActivationFunctionType, AxisListType
+
+F, B, H, I, U = "float32", "bfloat16", "float16", "int32", "uint16"
+SB = {
+    "X": (512, F), "gx": (128, F), "xq": (128, F), "mA": (32, F), "ci": (16, I), "cf": (16, F), "cc": (32, F),
+    "BD": (128, B), "BDh": (128, H), "BDdp": (128, B), "BDdn": (128, B), "BDo": (128, H), "BDo2": (128, B), "xm": (128, F), "xn": (128, F),
+    "ID": (128, B), "TRI": (128, B), "ONE": (128, B), "Tlo": (128, B), "x32": (512, B), "rI": (32, I), "offR": (32, U), "FH": (2048, H), "mq": (16, F),
+    "E64": (144, B), "Er0": (144, B), "En0": (144, B), "En1": (144, B), "En2": (144, B), "Es": (144, B), "Ek": (144, B), "Eo": (144, B),
+    "E1": (144, B), "Eth": (144, B), "Eh": (144, H),
+    "TA": (1024, H), "HX": (512, H), "mask": (1024, B), "tie": (256, B), "Mrow": (512, F), "x21": (512, F), "x613": (512, F),
+    "m21": (32, F), "m37": (32, F), "m613": (32, F), "mneg": (32, F), "cB": (16, F), "j16": (128, F),
+    "glI": (512, I), "LSp": (528, F), "offN": (512, U), "onb": (512, B), "C": (512, F), "C0": (512, F), "C1": (512, F), "GN": (8192, B), "T01": (528, B),
+    "nrow": (512, B), "ky": (512, F), "kyT": (512, F), "ks": (512, F), "kp": (512, F), "kI": (32, I), "khI": (32, I), "khH": (32, H), "klI": (32, I), "klH": (32, H),
+    "km0": (32, F), "km1": (32, F), "km2": (32, F), "c15m": (32, F),
+    "W": (4112, B), "nbI": (512, I), "vr0": (512, I), "vrh": (512, H), "thr": (256, I), "thI": (512, I), "thb": (512, B), "thB": (16, F), "thK": (16, F), "thT": (16, F),
+    "z0": (272, B), "z1": (272, B), "z2": (272, B), "z3": (256, B), "drow": (1024, B),
+    "dA": (32, F), "p4": (128, F), "pI": (256, I), "low": (128, B),
+    "gs0": (32, B), "gs1": (32, B), "gs2": (32, B), "gl0": (32, B), "gl1": (32, B), "gl2": (32, B),
+    "hs0": (32, B), "hs1": (32, B), "hs2": (32, B), "hl0": (32, B), "hl1": (32, B), "hl2": (32, B),
+    "sI": (512, I), "sF": (1024, F), "sU": (512, U), "eq": (512, B), "Zq": (512, B), "gr": (512, B), "gr2": (512, B), "prod": (512, H),
+    "G4": (2048, B), "D2": (1024, B), "tA": (64, F), "rowh": (64, H), "dlt": (512, B), "WK": (4608, B),
+    "GA": (4608, B), "GL": (4096, B), "sc": (4096, B), "offL": (256, U), "offM": (256, U), "zs": (256, B), "zI": (256, I), "lv": (1280, F), "lvI": (512, I),
+    "on16": (256, F), "hiT": (512, B), "yv": (512, B), "tk": (512, F), "kwI": (32, I), "wr": (256, B), "eqo": (256, B),
+    "sB": (256, F), "sBb": (64, B), "full": (16, B), "mk": (256, B), "jv": (16, H), "oX": (32, F), "lt": (2048, B), "rt": (512, B),
+}
+ALIAS = {}
+
+
+def share(to, names):
+    at = 0
+    for n in names:
+        ALIAS[n] = (to, at)
+        at += SB[n][0]
+    return at
+
+
+SCRATCH = {}
+for _to, _ns in (("aI", ("vr0", "nbI", "thr", "thI", "zI")), ("aB", ("onb", "thb")), ("aF", ("ks", "kp")),
+                 ("sm", ("m21", "m37", "m613", "mneg", "c15m", "km0", "km1", "km2", "oX", "dA", "tA", "mq", "cB", "thB", "thK", "thT")),
+                 ("smI", ("kI", "khI", "klI", "rI", "kwI")),
+                 ("EE", ("E64", "Er0", "En0", "En1", "En2", "Es", "Ek", "Eo", "E1", "Eth"))):
+    SCRATCH[_to] = ("sbuf", [128, share(_to, _ns)], SB[_ns[0]][1])
+for _n in SB:
+    if _n not in ALIAS:
+        SCRATCH[_n] = ("sbuf", [128, SB[_n][0]], SB[_n][1])
+for _b in range(8):
+    SCRATCH["b%d" % _b] = ("psum", [128, 512], F)
+SEMAPHORES = ["sV", "sS", "sP", "sG"] + ["d%d" % i for i in range(12)] + [a + str(t) for a in ("az", "ah", "ag", "lz", "lh", "lg") for t in range(3)]
+
+
+def rank_program(g, core, T, topo):
+    rank = T.rank_of(core)
+    if rank is None:
+        return
+    N = len(T.cores)
+    OP, AF = AluOpType, ActivationFunctionType
+    ADD, SUB, MUL, MAX, MIN = OP.add, OP.subtract, OP.mult, OP.max, OP.min
+    GT, GE, LT, LE, EQ = OP.is_gt, OP.is_ge, OP.is_lt, OP.is_le, OP.is_equal
+    SHR, AND = OP.arith_shift_right, OP.bitwise_and
+    eng = {"V": g.vector, "S": g.scalar, "P": g.tensor, "G": g, "D": g.sync}
+    hist, known, total, nd = {}, {q: {} for q in "VSPGD"}, {}, [0]
+    banks = ["b%d" % k for k in range(8)]
+
+    def order(q, acc):
+        toks = []
+        for (n, lo, hi), w in acc:
+            for r in hist.get(n, []):
+                if n in banks and r[3] != q:
+                    toks.append(r[4])
+                    continue
+                if not (lo < r[1] and r[0] < hi) or not (w or r[2]):
+                    continue
+                if r[3] == q == "P":
+                    continue
+                toks.append(r[4])
+        toks.sort(key=lambda k: -len(k[2]))
+        for i, (s, v, kn) in enumerate(toks):
+            if known[q].get(s, 0) >= v:
+                continue
+            if any(j != i and (k[2].get(s, 0) >= v and (k[0] != s or k[1] > v)) for j, k in enumerate(toks)):
+                continue
+            eng[q].wait_ge(T.sem[s], v)
+            for a, b in kn.items():
+                known[q][a] = max(known[q].get(a, 0), b)
+            known[q][s] = max(known[q].get(s, 0), v)
+
+    def note(q, acc, tok, dma=False):
+        for (n, lo, hi), w in acc:
+            keep = []
+            for r in hist.get(n, []):
+                inside = lo <= r[0] and r[1] <= hi
+                ps = n in banks
+                if inside and (w if not ps else (w or not r[2])) and not (ps and r[3] != q and not w):
+                    continue
+                if inside and not w and not r[2] and r[3] == q and not dma:
+                    continue
+                keep.append(r)
+            keep.append((lo, hi, w, "dma" if dma else q, tok))
+            hist[n] = keep
+
+    def emit(q, outs, ins, call):
+        acc = [(a, False) for v in ins if v is not None and not isinstance(v, (int, float)) for a in v[1]] + [(a, True) for a in outs[1]]
+        order(q, acc)
+        s = "s" + q
+        total[s] = total.get(s, 0) + 1
+        call(eng[q]).then_inc(T.sem[s], 1)
+        kn = dict(known[q])
+        kn[s] = total[s]
+        note(q, acc, (s, total[s], kn))
+
+    def a(n, lo=0, hi=None, st=1):
+        hi = SB[n][0] if hi is None and n in SB else 512 if hi is None else hi
+        if n in ALIAS:
+            o = ALIAS[n][1]
+            n, lo, hi = ALIAS[n][0], lo + o, hi + o
+        return (T[n][:, lo:hi:st] if st > 1 else T[n][:, lo:hi], [(n, lo, hi)])
+
+    def ind(w, o):
+        return (w[0].indirect(o[0]), w[1] + o[1])
+
+    def x(v):
+        return v if v is None or isinstance(v, (int, float)) else v[0]
+
+    def ts(o, i, s1, op0, s2=None, op1=None):
+        if op1 is None:
+            emit("V", o, [i, s1], lambda e: e.tensor_scalar(o[0], i[0], x(s1), None, op0))
+        else:
+            emit("V", o, [i, s1, s2], lambda e: e.tensor_scalar(o[0], i[0], x(s1), x(s2), op0, op1))
+
+    def tt(o, i, j, op):
+        emit("V", o, [i, j], lambda e: e.tensor_tensor(o[0], i[0], j[0], op))
+
+    def cp(o, i):
+        emit("V", o, [i], lambda e: e.tensor_copy(o[0], i[0]))
+
+    def fill(o, c):
+        emit("V", o, [], lambda e: e.memset(o[0], c))
+
+    def scan(o, d0, d1, init, op1):
+        emit("V", o, [d0, d1], lambda e: e.tensor_tensor_scan(o[0], d0[0], d1[0], init, MUL, op1))
+
+    def act(o, i, scale=1.0, bias=0.0, f=None):
+        f = (AF.Copy if bias == 0.0 else AF.Identity) if f is None else f
+        emit("S", o, [i, scale], lambda e: e.activation(o[0], i[0], f, bias=bias, scale=x(scale)))
+
+    def mm(o, l, r, start, stop):
+        emit("P", o, [l, r], lambda e: e.matmul(o[0], l[0], r[0], start, stop))
+
+    def iota(o, pat, base, cm):
+        emit("G", o, [], lambda e: e.iota(o[0], pat, base, cm, allow_small_or_imprecise_dtypes=True))
+
+    def dma(q, out, in_, acc):
+        order(q, acc)
+        s = "d%d" % nd[0]
+        nd[0] += 1
+        eng[q].dma_start(out, in_).then_inc(T.sem[s], 16)
+        total[s] = 16
+        kn = dict(known[q])
+        kn[s] = 16
+        note(q, acc, (s, 16, kn), True)
+
+    def es(E, q):
+        return a(E, 15 - q, 143 - q)
+
+    def conv(o, E, src, first=True, last=True):
+        for q in range(16):
+            mm(o, es(E, q), src(q), first and q == 0, last and q == 15)
+
+    def every(n, lo, hi):
+        return lambda q: a(n, lo + q, hi, 16)
+
+    def rows(bank, src, n, lo=0):
+        for q in range(16):
+            mm(a(bank, lo + q, lo + 16 * n, 16), a("FH", 128 * q, 128 * q + 128), src, True, True)
+
+    def send(dst, buf, rbuf, n, arr, loc):
+        to = T.cores[dst]
+        use = topo.engines(core, to)[:8]
+        rid, pid = topo.addr(to)[0], topo.addr(to)[1]
+        acc = [((buf, 0, n), False)]
+        order("G", acc)
+        g.remote_dma(T[rbuf][:, 0:n], T[buf][:, 0:n], T.sem[arr], T.sem[loc], pid, rid, sum(1 << e for e in use))
+        total[loc] = len(use)
+        note("G", acc, (loc, len(use), {loc: len(use)}), True)
+
+    def lands(src, buf, n, arr):
+        k = len(topo.engines(T.cores[src], core)[:8])
+        total[arr] = k
+        note("R", [((buf, 0, n), True)], (arr, k, {arr: k}), True)
+
+    up, dn = (rank + 1) % N, (rank - 1) % N
+    for t in range(3):
+        lands((rank - 1 - t) % N, "z%d" % (t + 1), 256, "az%d" % t)
+        lands(dn, "hl%d" % t, 32, "ah%d" % t)
+        lands(up, "gl%d" % t, 32, "ag%d" % t)
+
+    def load(q, v, src, part=None):
+        dma(q, v[0] if part is None else part, src, [(r, True) for r in v[1]])
+
+    load("D", a("glI"), T.gl[:, :])
+    iota(a("ci", 0, 1), [[0, 1]], 0, 1)
+    iota(a("gx"), [[1, 8], [0, 16]], 0, 0)
+    iota(a("X"), [[1, 512]], 0, 0)
+    load("S", a("W", 16), T.rec[:, :])
+    fill(a("vr0"), 0)
+    fill(a("thr"), 0)
+    load("D", a("vr0"), T.val[:, :], T["aI"][0:128:16, 0:512])
+    load("D", a("nbI"), T.nb[:, :])
+    load("D", a("z0", 0, 256), T.zl[:, :])
+    load("D", a("thr"), T.th[:, :], T["aI"][0:128:16, 1024:1280])
+    iota(a("mA"), [[16, 32]], 0, 1)
+    iota(a("xq"), [[0, 8], [1, 16]], 0, 0)
+    iota(a("tie"), [[-256, 16], [0, 16]], 3840, 0)
+    iota(a("x32"), [[0, 16], [1, 32]], 0, 0)
+    iota(a("rI"), [[1, 16], [0, 2]], 0, 0)
+    iota(a("WK", 512), [[0, 4096]], 0, 0)
+
+    for n, (op, c) in enumerate(((AND, 15), (AND, 112), (AND, 96), (SHR, 4), (AND, 14), (AND, 1), (AND, 7), (AND, 8))):
+        ts(a("ci", n + 1, n + 2), a("ci", 0, 1), c, op)
+    ts(a("ci", 9, 10), a("ci", 0, 1), 4, SHR, 1, AND)
+    cp(a("cf", 0, 10), a("ci", 0, 10))
+
+    def cf(n):
+        return a("cf", n, n + 1)
+
+    def cc(n):
+        return a("cc", n, n + 1)
+
+    def mk_e(n, w):
+        ts(a(n), a("X", 0, 144), cc(0), EQ, w, MUL)
+
+    ts(a("BD"), a("gx"), cf(4), EQ)
+    ts(cc(8), cf(1), 1.0, OP.not_equal)
+    ts(cc(7), cf(1), 0.0, OP.not_equal)
+    ts(cc(9), cc(8), 33.0, MUL, -32.0, ADD)
+    ts(cc(10), cc(7), 33.0, MUL, -32.0, ADD)
+    ts(cc(0), cf(2), 15.0, ADD)
+    ts(cc(2), cf(1), 2.0, EQ, 16384.0, MUL)
+    ts(cc(11), cf(1), -1024.0, MUL, 15359.0, ADD)
+    fill(a("T01", 0, 1), -32.0)
+    mk_e("En2", cc(2))
+    ts(a("LSp", 0, 512), a("glI"), 1.0, ADD)
+    act(a("onb"), a("LSp", 0, 512), f=AF.Sign)
+    ts(a("offN"), a("glI"), 1.0, ADD)
+    mm(a("b5"), a("BD"), a("onb"), True, True)
+    ts(a("T01", 1, 513, 2), a("b5", 0, 512, 2), cc(8), MUL, cc(9), ADD)
+    ts(a("T01", 2, 514, 2), a("b5", 1, 512, 2), cc(7), MUL, cc(10), ADD)
+
+    def gather_n(q, ch):
+        o, i = a("GN", 1024 * ch, 1024 * ch + 1024), ind(a("T01", 0, 513), a("offN", 64 * ch, 64 * ch + 64))
+        if q == "V":
+            cp(o, i)
+        else:
+            act(o, i)
+
+    def kmax_pe(bank, ch):
+        conv(a(bank, 128 * ch, 128 * ch + 128), "En2", every("GN", 2048 * ch, 2048 * ch + 2048))
+
+    def kmax_key(src, add, ch):
+        lo, hi = 128 * ch, 128 * ch + 128
+        if add is not None:
+            tt(a("ky", lo, hi), a(src, lo, hi), a(add, lo, hi), ADD)
+            src = "ky"
+        emit("V", a("kyT", lo, hi), [a(src, lo, hi)], lambda e: e.transpose(a("kyT", lo, hi)[0], a(src, lo, hi)[0]))
+        scan(a("ks", lo, hi), a("mask", 0, 128), a("kyT", lo, hi), 0.0, MAX)
+
+    def kmax_fin(small, so, dest):
+        cp(a("kI"), a("ks", 15, 512, 16))
+        ts(a("khI"), a("kI"), 10, SHR)
+        ts(a("klI"), a("kI"), 1023, AND)
+        cp(a("khH"), a("khI"))
+        cp(a("klH"), a("klI"))
+        for c1 in range(2):
+            n = 0
+            for g1 in range(2):
+                for part, src in ((1, "khH"), (0, "klH")):
+                    k = 128 * (4 * part + 2 * c1 + g1)
+                    mm(a(small, so + c1, so + 32, 2), a("TA", k, k + 128), a(src, g1, 32, 2), n == 0, n == 3)
+                    n += 1
+        return lambda: ts(a(dest), a(small, so, so + 32), 512.0, MAX)
+
+    for ch in range(1, 6):
+        gather_n("S", ch)
+    gather_n("V", 0)
+    fill(a("mask"), 1.0)
+    fill(a("mask", 0, 1024, 16), 0.0)
+    mk_e("Eh", 1.0)
+    cp(a("BDh"), a("BD"))
+    cp(a("vrh"), a("vr0"))
+    kmax_pe("b6", 0)
+    kmax_pe("b6", 1)
+    mm(a("b7"), a("BDh"), a("vrh"), True, True)
+    conv(a("b3", 0, 32), "Eh", every("vrh", 0, 512))
+    ts(a("C"), a("LSp", 0, 512), cc(11), ADD)
+    ts(a("lvI", 0, 512), a("glI"), 1, AND)
+    gather_n("V", 6)
+    ts(a("kp"), a("lvI", 0, 512), -524288.0, MUL)
+    gather_n("V", 7)
+    kmax_pe("b6", 2)
+    kmax_pe("b6", 3)
+    ts(a("mA"), a("mA"), cf(2), SUB)
+    for n, s, b, src in (("m21", 2.0, 1.0, "mA"), ("m37", 2.0, 37.0, "mA"), ("m613", 2.0, 613.0, "mA"), ("mneg", 1.0, -512.0, "mA"),
+                         ("Mrow", 1.0, 1.0, "X"), ("x613", 2.0, 613.0, "X"), ("x21", 2.0, 1.0, "X")):
+        act(a(n), a(src), s, b)
+    act(a("nrow"), a("b5"))
+    act(a("drow", 0, 512), a("b7"))
+    tt(a("C0"), a("C"), a("kp"), ADD)
+    for g1 in range(2):
+        ts(cc(16 + g1), cf(3), cf(1), ADD, 16.0 * g1, ADD)
+    ts(cc(18), cf(9), 0.0, EQ)
+    for c1, c in enumerate((cc(18), cf(9))):
+        ts(cc(20 + c1), c, 1024.0, MUL)
+        for g1 in range(2):
+            for part in range(2):
+                k = 128 * (4 * part + 2 * c1 + g1)
+                ts(a("TA", k, k + 128), a("X", 0, 128), cc(16 + g1), EQ, cc(20 + c1) if part else c, MUL)
+    cp(a("gs0"), a("b3", 0, 32))
+    cp(a("dA"), a("b3", 0, 32))
+    send(dn, "gs0", "gl0", 32, "ag0", "lg0")
+    ts(cc(1), cf(1), 0.0, EQ)
+    ts(cc(4), cf(1), 256.0, MUL, 1024.0, ADD)
+    mk_e("Er0", cc(1))
+    mk_e("Es", cc(4))
+    mk_e("E64", 64.0)
+    for ch in range(4):
+        kmax_key("b6", "C0", ch)
+    km0 = kmax_fin("b1", 0, "km0")
+    ts(a("kp"), a("kp"), -1.0, MUL, -524288.0, ADD)
+    km0()
+    later = [None, None]
+    fill(a("LSp", 512, 528), 0.0)
+    fill(a("drow", 512, 528), 0.0)
+    fill(a("W", 0, 16), 0.0)
+    fill(a("z0", 256, 272), 0.0)
+
+    def trial_tables():
+        for j in range(4):
+            ts(a("pI", 32 * j, 32 * j + 32), a("dA"), float(j), ADD)
+        ts(a("pI", 128, 256), a("pI", 0, 128), 15, AND)
+        cp(a("p4"), a("pI", 128, 256))
+        tt(a("low"), a("p4"), a("j16"), ADD)
+
+    def consts_a():
+        for j in range(4):
+            fill(a("j16", 32 * j, 32 * j + 32), 16.0 * j)
+        trial_tables()
+
+    def consts_a2():
+        tt(a("C1"), a("C"), a("kp"), ADD)
+        tt(a("kp"), a("b6"), a("C1"), ADD)
+        ts(a("ID"), a("X", 0, 128), cf(0), EQ)
+        ts(a("b0"), a("nbI"), 1.0, ADD)
+
+    def consts_b():
+        ts(a("mq"), a("X", 0, 16), cf(1), EQ)
+        for q in range(16):
+            ts(a("FH", 128 * q, 128 * q + 128), a("BD"), a("mq", q, q + 1), MUL)
+
+    def consts_c():
+        ts(a("xm"), a("xq"), 2.0, LT)
+        tt(a("BDdp"), a("xm"), a("BD"), MUL)
+        ts(a("BDdn"), a("BDdp"), -1.0, MUL)
+        ts(a("xm"), a("xq"), -2.5, ADD)
+        tt(a("xn"), a("xm"), a("xm"), MUL)
+        ts(a("xm"), a("xn"), 0.3, LT)
+        tt(a("BDo"), a("xm"), a("BD"), MUL)
+
+    def consts_d():
+        ts(cc(5), cf(5), 0.0, EQ, 4096.0, MUL)
+        ts(cc(6), cf(5), 2.0, EQ)
+        mk_e("Ek", cc(5))
+        mk_e("Eo", cc(6))
+        mk_e("E1", 1.0)
+        ts(a("BDo2"), a("BD"), cc(6), MUL)
+        fill(a("ONE"), 1.0)
+        ts(a("cB"), a("mA", 0, 16), 3840.0, ADD)
+        ts(a("xm"), a("X", 0, 128), cf(0), LT)
+        tt(a("TRI"), a("xm"), a("BD"), MUL)
+        ts(a("xm"), a("xq"), 1.0, ADD)
+        tt(a("xn"), a("xm"), a("BD"), MUL)
+        ts(a("Tlo"), a("xn"), -1.0, ADD)
+        cp(a("offR"), a("rI"))
+        ts(cc(22), cc(1), 64.0, MUL)
+        mk_e("Eth", cc(22))
+        ts(a("thI", 0, 256), a("thr"), 6, SHR)
+        ts(a("thI", 256, 512), a("thr"), 63, AND)
+        cp(a("thb"), a("thI"))
+        conv(a("b3", 64, 80), "Eth", every("thb", 0, 256), True, False)
+        conv(a("b3", 64, 80), "Er0", every("thb", 256, 512), False, True)
+        conv(a("b3", 96, 128), "Er0", every("nrow", 0, 512))
+
+    def consts_d2():
+        cp(a("thB"), a("b3", 64, 80))
+        ts(a("thK"), a("thB"), 4096.0, MUL, 4095.0, ADD)
+        ts(a("c15m"), a("b3", 96, 128), -1024.0, MUL, 15359.0, ADD)
+
+    def consts_e():
+        ts(cc(12), cf(7), 2.0, MUL, cf(2), ADD)
+        ts(cc(13), cc(12), 1.0, ADD)
+        ts(cc(14), cf(8), 0.0, EQ)
+        ts(cc(15), cf(8), 0.0, GT)
+        for t in range(2):
+            for h in range(2):
+                k = 128 * (2 * t + h)
+                ts(a("HX", k, k + 128), a("X", 0, 128), cc(12 + t), EQ, cc(14 + h), MUL)
+        ts(cc(3), cf(1), 1.0, EQ, 16384.0, MUL)
+        mk_e("En1", cc(3))
+        ts(cc(3), cf(1), 0.0, EQ, 16384.0, MUL)
+        mk_e("En0", cc(3))
+        for t in (1, 2):
+            fill(a("z%d" % t, 256, 272), 0.0)
+
+    def ghost_rows(src):
+        rows("b7", src, 32)
+        act(a("drow", 512, 1024), a("b7"))
+
+    def f(n):
+        return a("sF", 32 * n, 32 * n + 32)
+
+    def i(n):
+        return a("sI", 32 * n, 32 * n + 32)
+
+    def u(n, m=1):
+        return a("sU", 32 * n, 32 * (n + m))
+
+    for t in range(3):
+        par, zt = t & 1, "z%d" % t
+
+        def med(n, o=0, par=par):
+            return a(n, o + par, o + 512, 2)
+
+        if t == 0:
+            cp(i(0), a("km0"))
+        else:
+            tt(i(0), a("km%d" % t), f(31), MAX)
+        ts(i(1), i(0), 1023, AND)
+        cp(u(0), i(1))
+        ts(i(2), i(0), 1, SHR, 511, AND)
+        cp(u(2), i(2))
+        act(a("gr"), ind(a("drow", 0, 528), u(0)))
+        ts(f(0), i(1), 2.0, MUL, 1.0, ADD)
+        tt(a("eq"), ind(a("LSp"), u(0)), a("Mrow"), EQ)
+        act(a("Zq"), ind(a(zt), u(2)))
+        for j in range(4):
+            act(f(4 + j), f(0), 1.0, 612.0)
+        if t:
+            later[0]()
+        else:
+            consts_a()
+        if t == 1:
+            gather_n("S", 0)
+        conv(a("b1", 0, 32), "Er0", every("gr", 0, 512))
+        conv(a("b3", 0, 32), "Es", every("eq", 0, 512))
+        if t:
+            ghost_rows(a("rowh", 32, 64))
+        tt(i(3), f(0), a("mA"), MUL)
+        ts(i(4), i(3), 4, SHR, 4095, AND)
+        tt(f(1), i(4), a("mA"), ADD)
+        tt(a("sF", 256, 384), a("p4"), a("sF", 128, 256), MUL)
+        if t == 0:
+            consts_a2()
+        tt(a("prod"), a("b0"), a("eq"), MUL)
+        conv(a("b2", 0, 32), "Eh", every("prod", 0, 512))
+        conv(a("b4", 0, 16), "Er0", lambda q: a("nrow", 2 * q + par, 512, 32))
+        tt(f(3), a("b1", 0, 32), a("m37"), MUL)
+        tt(f(3), f(3), f(1), ADD)
+        for j in range(4):
+            tt(i(8 + j), f(8 + j), f(3), ADD)
+        ts(a("sI", 256, 384), a("sI", 256, 384), 4095, AND)
+        ts(u(4, 4), a("sI", 256, 384), 16.0, ADD)
+        ts(a("offL"), med("LSp"), -1.0, ADD)
+
+        def trial(j):
+            tt(a("G4", 512 * j, 512 * j + 512), ind(a("W"), u(4 + j)), a("Zq"), MAX)
+
+        def ga(ch):
+            act(a("GA", 512 + 1024 * ch, 1536 + 1024 * ch), ind(a("drow", 0, 512), a("offL", 64 * ch, 64 * ch + 64)))
+
+        act(a("lv", 0, 256), med("LSp"), 1.0, -1.0)
+        act(a("lv", 512, 768), med("LSp"), 2.0, 35.0)
+        act(a("on16"), med("LSp"), f=AF.Sign)
+        act(a("on16"), a("on16"), 8208.0, -8192.0)
+        if t == 1:
+            gather_n("S", 1)
+        ga(0)
+        trial(0)
+        trial(1)
+        if t == 0:
+            consts_b()
+            cp(a("rowh", 32, 64), a("gl0"))
+            ghost_rows(a("rowh", 32, 64))
+        ts(f(16), a("b2", 0, 32), -1.0, ADD, 0.0, MAX)
+        cp(u(8), f(16))
+        act(a("gr2"), ind(a("drow"), u(8)))
+        mm(a("b1", 64, 128), a("ID"), a("low", 0, 64), True, False)
+        conv(a("b1", 64, 128), "E64", every("G4", 0, 1024), False, True)
+        act(a("tA"), a("b1", 64, 128))
+        ga(1)
+        ts(f(2), i(2), -1024.0, ADD)
+        tt(f(17), a("b3", 0, 32), f(2), ADD)
+        ts(f(18), a("b3", 0, 32), 0.0, GT)
+        ts(f(26), a("b3", 0, 32), 1.0 / 256, MUL, 508.0, ADD)
+        ts(f(27), i(2), 16.0, MUL)
+        conv(a("b3", 32, 64), "Er0", every("gr2", 0, 512))
+        trial(2)
+        tt(f(17), f(17), a("mneg"), MAX)
+        tt(i(5), f(16), a("m21"), MUL)
+        ts(f(20), f(16), 2.0, MUL, 37.0, ADD)
+        ts(u(10), f(17), 512.0, ADD)
+        ts(i(5), i(5), 4, SHR, 4095, AND)
+        tt(f(22), a("dA"), f(20), MUL)
+        tt(f(26), f(26), f(27), ADD)
+        ts(a("full"), a("b4", 0, 16), 15.5, GT)
+        tt(f(26), f(26), f(18), MUL)
+        trial(3)
+        mm(a("b2", 64, 128), a("ID"), a("low", 64, 128), True, False)
+        conv(a("b2", 64, 128), "E64", every("G4", 1024, 2048), False, True)
+        if t == 0:
+            consts_c()
+        mm(a("b4"), a("BDo"), a("prod"), True, False)
+        ga(2)
+        ga(3)
+        tt(f(26), f(26), a("mA"), MAX)
+        tt(f(19), i(5), f(16), ADD)
+        cp(u(11), f(26))
+        tt(f(21), a("b3", 32, 64), a("m613"), MUL)
+        tt(f(19), f(19), f(21), ADD)
+        tt(i(6), f(22), f(19), ADD)
+        ts(i(6), i(6), 4095, AND)
+        ts(u(12), i(6), 16.0, ADD)
+        tt(a("D2", 0, 512), ind(a("W"), u(12)), a("Zq"), MAX)
+        mm(a("b4"), a("BDdn"), a("D2", 0, 512), False, False)
+        tt(a("tk", 0, 64), a("tA"), a("b2", 64, 128), MIN)
+        tt(i(7), a("tk", 0, 32), a("tk", 32, 64), MIN)
+        ts(i(7), i(7), 15, AND)
+        tt(f(23), i(7), f(20), MUL)
+        cp(a("rowh", 0, 32), i(7))
+        tt(i(12), f(23), f(19), ADD)
+        tt(f(24), i(7), a("dA"), SUB)
+        ts(i(12), i(12), 4095, AND)
+        ts(u(14), i(12), 16.0, ADD)
+        tt(a("D2", 512, 1024), ind(a("W"), u(14)), a("Zq"), MAX)
+        rows("b5", a("rowh", 0, 32), 32)
+        act(a("dlt"), a("b5"))
+        mm(a("b4"), a("BDdp"), a("D2", 512, 1024), False, True)
+        act(a("hiT"), a("b4"), cf(6))
+        if t == 1:
+            for ch in range(2, 6):
+                gather_n("S", ch)
+            kmax_pe("b5", 0)
+        tt(f(24), f(24), f(18), MUL)
+        tt(f(25), a("dA"), f(24), ADD)
+        if t < 2:
+            cp(a("gs%d" % (t + 1)), f(25))
+            send(dn, "gs%d" % (t + 1), "gl%d" % (t + 1), 32, "ag%d" % (t + 1), "lg%d" % (t + 1))
+        ts(a("mk"), med("nrow"), cf(1), EQ)
+        tt(a("lvI", 0, 256), a("lv", 0, 256), med("x21"), MUL)
+        ts(a("lvI", 0, 256), a("lvI", 0, 256), 4, SHR, 4095, AND)
+        cp(ind(a("GA"), u(11)), a("dlt"))
+        conv(a("b6", 0, 256), "Er0", every("GA", 512, 4608))
+        tt(a("yv"), a("b4"), a("hiT"), SUB)
+        cp(ind(a("WK"), u(10)), a("yv"))
+        if t == 0:
+            consts_d()
+        mm(a("b7", 0, 256), a("ID"), a("tie"), True, False)
+        conv(a("b7", 0, 256), "Ek", every("WK", 512, 4608), False, True)
+        tt(a("lv", 256, 512), a("lvI", 0, 256), a("lv", 0, 256), ADD)
+        tt(a("lv", 768, 1024), a("lv", 512, 768), med("drow"), MUL)
+        tt(a("lv", 256, 512), a("lv", 256, 512), a("lv", 768, 1024), ADD)
+        tt(a("b6", 256, 512), a("b6", 0, 256), med("x613"), MUL)
+        tt(a("lvI", 256, 512), a("b6", 256, 512), a("lv", 256, 512), ADD)
+        ts(a("lvI", 256, 512), a("lvI", 256, 512), 4095, AND)
+        tt(a("lv", 768, 1024), a("lvI", 256, 512), a("on16"), ADD)
+        cp(a("offM"), a("lv", 768, 1024))
+        for ch in range(4):
+            act(a("GL", 1024 * ch, 1024 * ch + 1024), ind(a("W"), a("offM", 64 * ch, 64 * ch + 64)))
+
+        def level_scan(ch):
+            lo = 1024 * ch
+            scan(a("sc", lo, lo + 1024), a("mask"), a("GL", lo, lo + 1024), 0.0, MAX)
+
+        if t == 0:
+            consts_d2()
+            for ch in range(4):
+                kmax_key("kp", None, ch)
+            later[1] = kmax_fin("b1", 224, "km1")
+        elif t == 1:
+            gather_n("S", 6)
+            gather_n("S", 7)
+            kmax_key("b5", "C0", 0)
+        cp(a("tk", 64, 192), a("b7", 128, 256))
+        tt(a("tk", 192, 320), a("b7", 0, 128), a("tk", 64, 192), MAX)
+        tt(a("tk", 320, 384), a("tk", 192, 256), a("tk", 256, 320), MAX)
+        tt(a("tk", 384, 416), a("tk", 320, 352), a("tk", 352, 384), MAX)
+        tt(a("kwI", 0, 16), a("tk", 384, 400), a("tk", 400, 416), MAX)
+        ts(a("kwI", 16, 32), a("kwI", 0, 16), 3840, AND)
+        tt(a("sB", 0, 16), a("cB"), a("kwI", 16, 32), SUB)
+        cp(a("sU", 480, 496), a("sB", 0, 16))
+        cp(a("wr"), ind(a("WK", 512, 4608), a("sU", 480, 496)))
+        tt(a("sB", 16, 32), a("kwI", 0, 16), a("thK"), GT)
+        cp(a("sBb", 0, 16), a("sB", 16, 32))
+        conv(a("b1", 128, 144), "Eo", every("wr", 0, 256))
+        mm(a("b4", 0, 256), a("BDo2"), a("wr"), True, True)
+        if t < 2:
+            mm(a("b3", 128, 144), a("ONE"), a("sBb", 0, 16), True, True)
+        level_scan(0)
+        tt(a("sB", 32, 48), a("b1", 128, 144), a("sB", 16, 32), MUL)
+        ts(a("sBb", 16, 32), a("sB", 32, 48), 512.5, GT)
+        mm(a("b2", 128, 144), a("BD"), a("sBb", 16, 32), True, True)
+        mm(a("b2", 144, 160), a("TRI"), a("sBb", 16, 32), True, True)
+        tt(a("eqo"), med("LSp"), a("b4", 0, 256), EQ)
+        mm(a("b1", 192, 208), a("ID"), a("full"), True, False)
+        conv(a("b1", 192, 208), "E1", every("eqo", 0, 256), False, True)
+        if t == 1:
+            kmax_pe("b5", 1)
+        ts(a("sB", 48, 64), a("sB", 32, 48), -512.0, ADD, 0.0, MAX)
+        scan(a("sB", 64, 80), a("ONE", 0, 16), a("b2", 128, 144), -60.0, ADD)
+        tt(a("sB", 80, 96), a("sB", 64, 80), a("b2", 144, 160), LE)
+        tt(a("sB", 96, 112), a("sB", 80, 96), a("sB", 48, 64), MUL)
+        ts(a("kwI", 0, 16), a("sB", 96, 112), -1.0, ADD)
+        ts(a("kwI", 16, 32), a("kwI", 0, 16), 15, AND)
+        ts(a("kwI", 0, 16), a("kwI", 0, 16), 4, SHR)
+        cp(a("sB", 112, 144), a("kwI", 0, 32))
+        tt(a("rt"), ind(a("sB", 112, 128), a("offR")), a("x32"), EQ)
+        for h in range(16):
+            ts(a("lt", 128 * h, 128 * h + 128), a("Tlo"), a("sB", 128 + h, 129 + h), EQ)
+            mm(a("b2", 192, 224), a("lt", 128 * h, 128 * h + 128), a("rt", 32 * h, 32 * h + 32), h == 0, h == 15)
+        ts(a("sB", 144, 160), a("sB", 32, 48), 512.5, LT)
+        cp(a("hs%d" % t), a("b2", 192, 224))
+        send(up, "hs%d" % t, "hl%d" % t, 32, "ah%d" % t, "lh%d" % t)
+        tt(a("sB", 144, 160), a("sB", 144, 160), a("b1", 192, 208), GT)
+        tt(a("jv"), a("sB", 144, 160), a("sB", 32, 48), MUL)
+        if t == 0:
+            consts_e()
+        if t < 2:
+            for h in range(2):
+                k = 128 * (2 * par + h)
+                mm(a("b3", 160 + h, 192, 2), a("HX", k, k + 128), a("jv"), True, True)
+        if t == 1:
+            kmax_key("b5", "C0", 1)
+            kmax_pe("b5", 2)
+        level_scan(1)
+        if t < 2:
+            if t == 0:
+                cp(a("oX"), a("b3", 160, 192))
+            else:
+                tt(a("oX"), a("oX"), a("b3", 160, 192), ADD)
+            cp(u(14), a("oX"))
+            act(a("gr"), ind(a("T01", 0, 513), u(14)))
+            tt(f(30), a("oX"), a("c15m"), ADD)
+            tt(i(13), a("gl%d" % (t + 1)), a("hs%d" % t), ADD)
+            ts(i(14), i(13), 15, AND)
+            cp(a("rowh", 32, 64), i(14))
+        level_scan(2)
+        level_scan(3)
+        mm(a("b6", 256, 512), a("ID"), a(zt, 0, 256), True, False)
+        mm(a("b6", 256, 512), a("ID"), a("sc", 15, 4096, 16), False, True)
+        if t == 1:
+            kmax_key("b5", "C0", 2)
+        ts(a("zI"), a("b6", 256, 512), 0.5, MUL, -0.25, ADD)
+        cp(a("zs"), a("zI"))
+        send((rank + 1 + t) % N, "zs", "z%d" % (t + 1), 256, "az%d" % t, "lz%d" % t)
+
+        def lists(t=t, med=med):
+            tt(a("lv", 1024, 1280), a("b2", 256, 512), a("mk"), MUL)
+            tt(med("LSp"), med("LSp"), a("lv", 1024, 1280), ADD)
+            if t == 0:
+                ts(a("lv", 1024, 1280), a("b2", 256, 512), 0.5, GT)
+                tt(a("nrow", 0, 512, 2), a("nrow", 0, 512, 2), a("lv", 1024, 1280), ADD)
+                ts(a("T01", 1, 513, 2), a("nrow", 0, 512, 2), cc(8), MUL, cc(9), ADD)
+            if t < 2:
+                emit("V", a("sB", 160, 161), [a("b3", 128, 144)], lambda e: e.tensor_reduce(a("sB", 160, 161)[0], a("b3", 128, 144)[0], axis=AxisListType.X, op=ADD))
+                cp(a("kwI", 0, 1), a("sB", 160, 161))
+                ts(a("kwI", 1, 2), a("kwI", 0, 1), 31, AND)
+                cp(a("sB", 161, 162), a("kwI", 1, 2))
+                ts(a("thT"), a("thB"), a("sB", 161, 162), ADD, 4080.0, MIN)
+                ts(a("thK"), a("thT"), 4096.0, MUL, 4095.0, ADD)
+
+        if t < 2:
+            later[0] = lists
+            conv(a("b3", 192, 224), "En1" if t == 0 else "En0", every("gr", 0, 512))
+            iota(a("WK", 512), [[0, 4096]], 0, 0)
+        else:
+            rows("b2", a("jv"), 16, 256)
+            lists()
+            ts(a("ky"), a("LSp", 0, 512), -1.0, ADD)
+            dma("D", T.yl[:, :], a("ky")[0], [(("ky", 0, 512), False)])
+        tt(i(13), f(25), a("hl%d" % t), ADD)
+        ts(i(14), i(13), 15, AND)
+        cp(a("rowh", 0, 32), i(14))
+        rows("b4", a("rowh", 0, 32), 32)
+        if t < 2:
+            tt(f(31), f(30), a("b3", 192, 224), ADD)
+            if t == 0:
+                later[1]()
+            act(a("drow", 0, 512), a("b4"))
+            if t == 1:
+                kmax_pe("b5", 3)
+            cp(a("dA"), i(14))
+            trial_tables()
+            if t == 1:
+                kmax_key("b5", "C0", 3)
+                km2 = kmax_fin("b1", 224, "km2")
+            rows("b2", a("jv"), 16, 256)
+            if t == 1:
+                km2()
+        else:
+            act(a("kyT"), a("b4"))
+            dma("D", T.yd[:, :], T.kyT[0:128:16, :], [(("kyT", 0, 512), False)])
+            dma("D", T.yz[:, :], T.z3[:, :], [(("z3", 0, 256), False)])
+    for s, v in total.items():
+        g.wait_ge(T.sem[s], v)

@@ -2,13 +2,13 @@ from concourse.mybir import AluOpType, ActivationFunctionType, AxisListType
 
 F, B, H, I, U = "float32", "bfloat16", "float16", "int32", "uint16"
 SB = {
-    "X": (512, F), "gx": (128, F), "xq": (128, F), "mA": (32, F), "ci": (16, I), "cf": (16, F), "cc": (32, F),
-    "BD": (128, B), "BDh": (128, H), "BDdp": (128, B), "BDdn": (128, B), "BDo": (128, H), "BDo2": (128, B), "xm": (128, F), "xn": (128, F),
-    "ID": (128, B), "TRI": (128, B), "ONE": (128, B), "Tlo": (128, B), "x32": (512, B), "rI": (32, I), "offR": (32, U), "FH": (2048, H), "mq": (16, F),
+    "X": (512, F), "gx": (128, F), "mA": (32, F), "ci": (16, I), "cf": (16, F), "cc": (32, F),
+    "BD": (128, B), "BDh": (128, H), "BDdp": (128, B), "BDdn": (128, B), "BDo": (128, H), "BDo2": (128, B), "BDt": (128, B),
+    "ID": (128, B), "TRI": (128, B), "ones": (2048, B), "Tlo": (128, B), "x32": (512, B), "rI": (32, I), "offR": (32, U), "FH": (2048, B),
     "E64": (144, B), "Er0": (144, B), "En0": (144, B), "En1": (144, B), "En2": (144, B), "Es": (144, B), "Ek": (144, B), "Eo": (144, B),
     "E1": (144, B), "Eth": (144, B), "Eh": (144, H),
     "TA": (1024, H), "HX": (512, H), "mask": (1024, B), "tie": (256, B), "Mrow": (512, F), "x21": (512, F), "x613": (512, F),
-    "m21": (32, F), "m37": (32, F), "m613": (32, F), "mneg": (32, F), "cB": (16, F), "j16": (128, F),
+    "m21": (32, F), "m37": (32, F), "m613": (32, F), "mneg": (32, F), "cB": (16, F),
     "glI": (512, I), "LSp": (528, F), "offN": (512, U), "onb": (512, B), "C": (512, F), "C0": (512, F), "C1": (512, F), "GN": (8192, B), "T01": (528, B),
     "nrow": (512, B), "ky": (512, F), "kyT": (512, F), "ks": (512, F), "kp": (512, F), "kI": (32, I), "khI": (32, I), "khH": (32, H), "klI": (32, I), "klH": (32, H),
     "km0": (32, F), "km1": (32, F), "km2": (32, F), "c15m": (32, F),
@@ -18,10 +18,10 @@ SB = {
     "gs0": (32, B), "gs1": (32, B), "gs2": (32, B), "gl0": (32, B), "gl1": (32, B), "gl2": (32, B),
     "hs0": (32, B), "hs1": (32, B), "hs2": (32, B), "hl0": (32, B), "hl1": (32, B), "hl2": (32, B),
     "sI": (512, I), "sF": (1024, F), "sU": (512, U), "eq": (512, B), "Zq": (512, B), "gr": (512, B), "gr2": (512, B), "prod": (512, H),
-    "G4": (2048, B), "D2": (1024, B), "tA": (64, F), "rowh": (64, H), "dlt": (512, B), "WK": (4608, B),
-    "GA": (4608, B), "GL": (4096, B), "sc": (4096, B), "offL": (256, U), "offM": (256, U), "zs": (256, B), "zI": (256, I), "lv": (1280, F), "lvI": (512, I),
-    "on16": (256, F), "hiT": (512, B), "yv": (512, B), "tk": (512, F), "kwI": (32, I), "wr": (256, B), "eqo": (256, B),
-    "sB": (256, F), "sBb": (64, B), "full": (16, B), "mk": (256, B), "jv": (16, H), "oX": (32, F), "lt": (2048, B), "rt": (512, B),
+    "G4": (2048, B), "D2": (1024, B), "tA": (64, F), "rowh": (64, B), "dlt": (512, B), "WK": (4608, B),
+    "GA": (4608, B), "GL": (4096, B), "sc": (4096, B), "offL": (256, U), "offM": (256, U), "zs": (256, B), "zf": (256, F), "lv": (1280, F), "lvI": (512, I),
+    "on16": (256, F), "hiT": (512, B), "yv": (512, B), "tk": (512, F), "kwI": (32, I), "wr": (256, B), "eqo": (256, B), "sg": (256, B),
+    "sB": (256, F), "sBb": (64, B), "full": (16, B), "mk": (512, B), "jv": (16, H), "jw": (48, B), "oX": (32, F), "lt": (2048, B), "rt": (512, B),
 }
 ALIAS = {}
 
@@ -35,8 +35,8 @@ def share(to, names):
 
 
 SCRATCH = {}
-for _to, _ns in (("aI", ("vr0", "nbI", "thr", "thI", "zI")), ("aB", ("onb", "thb")), ("aF", ("ks", "kp")),
-                 ("sm", ("m21", "m37", "m613", "mneg", "c15m", "km0", "km1", "km2", "oX", "dA", "tA", "mq", "cB", "thB", "thK", "thT")),
+for _to, _ns in (("aI", ("vr0", "nbI", "thr", "thI")), ("aB", ("onb", "thb")), ("aF", ("ks", "kp")),
+                 ("sm", ("m21", "m37", "m613", "mneg", "c15m", "km0", "km1", "km2", "oX", "dA", "tA", "cB", "thB", "thK", "thT")),
                  ("smI", ("kI", "khI", "klI", "rI", "kwI")),
                  ("EE", ("E64", "Er0", "En0", "En1", "En2", "Es", "Ek", "Eo", "E1", "Eth"))):
     SCRATCH[_to] = ("sbuf", [128, share(_to, _ns)], SB[_ns[0]][1])
@@ -149,6 +149,9 @@ def rank_program(g, core, T, topo):
     def iota(o, pat, base, cm):
         emit("G", o, [], lambda e: e.iota(o[0], pat, base, cm, allow_small_or_imprecise_dtypes=True))
 
+    def keep(o, i, pat, op, base, cm, c=0.0):
+        emit("G", o, [i], lambda e: e.affine_select(o[0], i[0], pat, op, c, base, cm))
+
     def dma(q, out, in_, acc):
         order(q, acc)
         s = "d%d" % nd[0]
@@ -169,9 +172,12 @@ def rank_program(g, core, T, topo):
     def every(n, lo, hi):
         return lambda q: a(n, lo + q, hi, 16)
 
-    def rows(bank, src, n, lo=0):
+    def rows(bank, src, n, lo=0, rest=None):
         for q in range(16):
-            mm(a(bank, lo + q, lo + 16 * n, 16), a("FH", 128 * q, 128 * q + 128), src, True, True)
+            o, w = a(bank, lo + q, lo + 16 * n, 16), a("FH", 128 * q, 128 * q + 128)
+            mm(o, w, src, True, rest is None)
+            if rest is not None:
+                mm(o, w, rest, False, True)
 
     def send(dst, buf, rbuf, n, arr, loc):
         to = T.cores[dst]
@@ -208,12 +214,17 @@ def rank_program(g, core, T, topo):
     load("D", a("nbI"), T.nb[:, :])
     load("D", a("z0", 0, 256), T.zl[:, :])
     load("D", a("thr"), T.th[:, :], T["aI"][0:128:16, 1024:1280])
+    iota(a("ones"), [[0, 2048]], 1, 0)
+    keep(a("mask"), a("ones", 0, 1024), [[0, 64], [1, 16]], GT, 0, 0)
     iota(a("mA"), [[16, 32]], 0, 1)
-    iota(a("xq"), [[0, 8], [1, 16]], 0, 0)
     iota(a("tie"), [[-256, 16], [0, 16]], 3840, 0)
     iota(a("x32"), [[0, 16], [1, 32]], 0, 0)
     iota(a("rI"), [[1, 16], [0, 2]], 0, 0)
-    iota(a("WK", 512), [[0, 4096]], 0, 0)
+    keep(a("ID"), a("ones", 0, 128), [[-1, 128]], EQ, 0, 1)
+    keep(a("FH"), a("ones"), [[-1, 16], [-16, 8], [0, 16]], EQ, 0, 1)
+    iota(a("Tlo"), [[0, 8], [1, 16]], 0, 0)
+    keep(a("Tlo"), a("Tlo"), [[-16, 8], [0, 16]], GE, 0, 1, -1.0)
+    keep(a("Tlo"), a("Tlo"), [[16, 8], [0, 16]], GE, 15, -1, -1.0)
 
     for n, (op, c) in enumerate(((AND, 15), (AND, 112), (AND, 96), (SHR, 4), (AND, 14), (AND, 1), (AND, 7), (AND, 8))):
         ts(a("ci", n + 1, n + 2), a("ci", 0, 1), c, op)
@@ -230,6 +241,10 @@ def rank_program(g, core, T, topo):
         ts(a(n), a("X", 0, 144), cc(0), EQ, w, MUL)
 
     ts(a("BD"), a("gx"), cf(4), EQ)
+    keep(a("BDdp"), a("BD"), [[0, 8], [-1, 16]], GE, 1, 0)
+    keep(a("BDt"), a("BD"), [[0, 8], [1, 16]], GE, -2, 0)
+    keep(a("BDt"), a("BDt"), [[0, 8], [-1, 16]], GE, 3, 0)
+    keep(a("TRI"), a("BD"), [[-1, 128]], GT, 0, 1)
     ts(cc(8), cf(1), 1.0, OP.not_equal)
     ts(cc(7), cf(1), 0.0, OP.not_equal)
     ts(cc(9), cc(8), 33.0, MUL, -32.0, ADD)
@@ -281,30 +296,31 @@ def rank_program(g, core, T, topo):
 
     for ch in range(1, 6):
         gather_n("S", ch)
-    gather_n("V", 0)
-    fill(a("mask"), 1.0)
-    fill(a("mask", 0, 1024, 16), 0.0)
+    for ch in (0, 6, 7):
+        gather_n("V", ch)
+    ts(a("mA"), a("mA"), cf(2), SUB)
+    mk_e("E1", 1.0)
+    kmax_pe("b6", 0)
+    kmax_pe("b6", 1)
+    kmax_pe("b4", 3)
+    kmax_pe("b4", 2)
+    ts(a("C"), a("LSp", 0, 512), cc(11), ADD)
+    ts(a("lvI", 0, 512), a("glI"), 1, AND)
+    ts(a("kp"), a("lvI", 0, 512), -524288.0, MUL)
+    tt(a("C0"), a("C"), a("kp"), ADD)
+    kmax_key("b6", "C0", 0)
+    kmax_key("b6", "C0", 1)
     mk_e("Eh", 1.0)
     cp(a("BDh"), a("BD"))
     cp(a("vrh"), a("vr0"))
-    kmax_pe("b6", 0)
-    kmax_pe("b6", 1)
     mm(a("b7"), a("BDh"), a("vrh"), True, True)
     conv(a("b3", 0, 32), "Eh", every("vrh", 0, 512))
-    ts(a("C"), a("LSp", 0, 512), cc(11), ADD)
-    ts(a("lvI", 0, 512), a("glI"), 1, AND)
-    gather_n("V", 6)
-    ts(a("kp"), a("lvI", 0, 512), -524288.0, MUL)
-    gather_n("V", 7)
-    kmax_pe("b6", 2)
-    kmax_pe("b6", 3)
-    ts(a("mA"), a("mA"), cf(2), SUB)
     for n, s, b, src in (("m21", 2.0, 1.0, "mA"), ("m37", 2.0, 37.0, "mA"), ("m613", 2.0, 613.0, "mA"), ("mneg", 1.0, -512.0, "mA"),
                          ("Mrow", 1.0, 1.0, "X"), ("x613", 2.0, 613.0, "X"), ("x21", 2.0, 1.0, "X")):
         act(a(n), a(src), s, b)
     act(a("nrow"), a("b5"))
     act(a("drow", 0, 512), a("b7"))
-    tt(a("C0"), a("C"), a("kp"), ADD)
+    act(a("C1"), a("kp"), -2.0, -524288.0)
     for g1 in range(2):
         ts(cc(16 + g1), cf(3), cf(1), ADD, 16.0 * g1, ADD)
     ts(cc(18), cf(9), 0.0, EQ)
@@ -314,20 +330,23 @@ def rank_program(g, core, T, topo):
             for part in range(2):
                 k = 128 * (4 * part + 2 * c1 + g1)
                 ts(a("TA", k, k + 128), a("X", 0, 128), cc(16 + g1), EQ, cc(20 + c1) if part else c, MUL)
-    cp(a("gs0"), a("b3", 0, 32))
-    cp(a("dA"), a("b3", 0, 32))
-    send(dn, "gs0", "gl0", 32, "ag0", "lg0")
+    kmax_key("b4", "C0", 3)
+    kmax_key("b4", "C0", 2)
+    km0 = kmax_fin("b1", 0, "km0")
     ts(cc(1), cf(1), 0.0, EQ)
     ts(cc(4), cf(1), 256.0, MUL, 1024.0, ADD)
-    mk_e("Er0", cc(1))
-    mk_e("Es", cc(4))
-    mk_e("E64", 64.0)
-    for ch in range(4):
-        kmax_key("b6", "C0", ch)
-    km0 = kmax_fin("b1", 0, "km0")
-    ts(a("kp"), a("kp"), -1.0, MUL, -524288.0, ADD)
+    ts(cc(5), cf(5), 0.0, EQ, 4096.0, MUL)
+    ts(cc(6), cf(5), 2.0, EQ)
+    ts(cc(22), cc(1), 64.0, MUL)
+    ts(cc(3), cf(1), 1.0, EQ, 16384.0, MUL)
+    ts(cc(23), cc(1), 16384.0, MUL)
+    act(a("Er0"), a("E1"), cc(1))
     km0()
-    later = [None, None]
+    cp(a("dA"), a("b3", 0, 32))
+    cp(a("gs0"), a("dA"))
+    send(dn, "gs0", "gl0", 32, "ag0", "lg0")
+    iota(a("WK", 512), [[0, 4096]], 0, 0)
+    later = [None] * 4
     fill(a("LSp", 512, 528), 0.0)
     fill(a("drow", 512, 528), 0.0)
     fill(a("W", 0, 16), 0.0)
@@ -338,61 +357,19 @@ def rank_program(g, core, T, topo):
             ts(a("pI", 32 * j, 32 * j + 32), a("dA"), float(j), ADD)
         ts(a("pI", 128, 256), a("pI", 0, 128), 15, AND)
         cp(a("p4"), a("pI", 128, 256))
-        tt(a("low"), a("p4"), a("j16"), ADD)
 
-    def consts_a():
-        for j in range(4):
-            fill(a("j16", 32 * j, 32 * j + 32), 16.0 * j)
-        trial_tables()
-
-    def consts_a2():
-        tt(a("C1"), a("C"), a("kp"), ADD)
-        tt(a("kp"), a("b6"), a("C1"), ADD)
-        ts(a("ID"), a("X", 0, 128), cf(0), EQ)
-        ts(a("b0"), a("nbI"), 1.0, ADD)
-
-    def consts_b():
-        ts(a("mq"), a("X", 0, 16), cf(1), EQ)
-        for q in range(16):
-            ts(a("FH", 128 * q, 128 * q + 128), a("BD"), a("mq", q, q + 1), MUL)
-
-    def consts_c():
-        ts(a("xm"), a("xq"), 2.0, LT)
-        tt(a("BDdp"), a("xm"), a("BD"), MUL)
-        ts(a("BDdn"), a("BDdp"), -1.0, MUL)
-        ts(a("xm"), a("xq"), -2.5, ADD)
-        tt(a("xn"), a("xm"), a("xm"), MUL)
-        ts(a("xm"), a("xn"), 0.3, LT)
-        tt(a("BDo"), a("xm"), a("BD"), MUL)
-
-    def consts_d():
-        ts(cc(5), cf(5), 0.0, EQ, 4096.0, MUL)
-        ts(cc(6), cf(5), 2.0, EQ)
-        mk_e("Ek", cc(5))
-        mk_e("Eo", cc(6))
-        mk_e("E1", 1.0)
-        ts(a("BDo2"), a("BD"), cc(6), MUL)
-        fill(a("ONE"), 1.0)
-        ts(a("cB"), a("mA", 0, 16), 3840.0, ADD)
-        ts(a("xm"), a("X", 0, 128), cf(0), LT)
-        tt(a("TRI"), a("xm"), a("BD"), MUL)
-        ts(a("xm"), a("xq"), 1.0, ADD)
-        tt(a("xn"), a("xm"), a("BD"), MUL)
-        ts(a("Tlo"), a("xn"), -1.0, ADD)
-        cp(a("offR"), a("rI"))
-        ts(cc(22), cc(1), 64.0, MUL)
-        mk_e("Eth", cc(22))
+    def consts_t():
         ts(a("thI", 0, 256), a("thr"), 6, SHR)
         ts(a("thI", 256, 512), a("thr"), 63, AND)
         cp(a("thb"), a("thI"))
-        conv(a("b3", 64, 80), "Eth", every("thb", 0, 256), True, False)
-        conv(a("b3", 64, 80), "Er0", every("thb", 256, 512), False, True)
-        conv(a("b3", 96, 128), "Er0", every("nrow", 0, 512))
+        conv(a("b5", 64, 80), "Eth", every("thb", 0, 256), True, False)
+        conv(a("b5", 64, 80), "Er0", every("thb", 256, 512), False, True)
+        conv(a("b5", 96, 128), "Er0", every("nrow", 0, 512))
 
-    def consts_d2():
-        cp(a("thB"), a("b3", 64, 80))
+    def consts_d():
+        cp(a("thB"), a("b5", 64, 80))
         ts(a("thK"), a("thB"), 4096.0, MUL, 4095.0, ADD)
-        ts(a("c15m"), a("b3", 96, 128), -1024.0, MUL, 15359.0, ADD)
+        ts(a("c15m"), a("b5", 96, 128), -1024.0, MUL, 15359.0, ADD)
 
     def consts_e():
         ts(cc(12), cf(7), 2.0, MUL, cf(2), ADD)
@@ -403,10 +380,6 @@ def rank_program(g, core, T, topo):
             for h in range(2):
                 k = 128 * (2 * t + h)
                 ts(a("HX", k, k + 128), a("X", 0, 128), cc(12 + t), EQ, cc(14 + h), MUL)
-        ts(cc(3), cf(1), 1.0, EQ, 16384.0, MUL)
-        mk_e("En1", cc(3))
-        ts(cc(3), cf(1), 0.0, EQ, 16384.0, MUL)
-        mk_e("En0", cc(3))
         for t in (1, 2):
             fill(a("z%d" % t, 256, 272), 0.0)
 
@@ -439,28 +412,45 @@ def rank_program(g, core, T, topo):
         cp(u(2), i(2))
         act(a("gr"), ind(a("drow", 0, 528), u(0)))
         ts(f(0), i(1), 2.0, MUL, 1.0, ADD)
+        ts(a("offL"), med("LSp"), -1.0, ADD)
         tt(a("eq"), ind(a("LSp"), u(0)), a("Mrow"), EQ)
-        act(a("Zq"), ind(a(zt), u(2)))
+        if t == 0:
+            act(a("Zq"), ind(a(zt), u(2)))
+
+        def ga(ch):
+            act(a("GA", 512 + 1024 * ch, 1536 + 1024 * ch), ind(a("drow", 0, 512), a("offL", 64 * ch, 64 * ch + 64)))
+
+        if t == 0:
+            for n, c in (("Es", cc(4)), ("E64", 64.0), ("Eth", cc(22))):
+                act(a(n), a("E1"), c)
+            trial_tables()
         for j in range(4):
             act(f(4 + j), f(0), 1.0, 612.0)
+        act(f(2), f(0), 0.25, -1024.25 - 0.5 * par)
+        act(f(27), f(0), 4.0, -4.0 - 8.0 * par)
+        for j in range(4):
+            act(a("low", 32 * j, 32 * j + 32), a("p4", 32 * j, 32 * j + 32), 1.0, 16.0 * j)
+        if t:
+            act(a("Zq"), ind(a(zt), u(2)))
+        if t != 1:
+            ga(0)
+        else:
+            gather_n("S", 1)
         if t:
             later[0]()
-        else:
-            consts_a()
-        if t == 1:
-            gather_n("S", 0)
         conv(a("b1", 0, 32), "Er0", every("gr", 0, 512))
         conv(a("b3", 0, 32), "Es", every("eq", 0, 512))
-        if t:
-            ghost_rows(a("rowh", 32, 64))
         tt(i(3), f(0), a("mA"), MUL)
         ts(i(4), i(3), 4, SHR, 4095, AND)
         tt(f(1), i(4), a("mA"), ADD)
         tt(a("sF", 256, 384), a("p4"), a("sF", 128, 256), MUL)
         if t == 0:
-            consts_a2()
+            tt(a("kp"), a("ky"), a("C1"), ADD)
+            ts(a("b0"), a("nbI"), 1.0, ADD)
         tt(a("prod"), a("b0"), a("eq"), MUL)
         conv(a("b2", 0, 32), "Eh", every("prod", 0, 512))
+        if t:
+            ghost_rows(a("rowh", 32, 64))
         conv(a("b4", 0, 16), "Er0", lambda q: a("nrow", 2 * q + par, 512, 32))
         tt(f(3), a("b1", 0, 32), a("m37"), MUL)
         tt(f(3), f(3), f(1), ADD)
@@ -468,39 +458,31 @@ def rank_program(g, core, T, topo):
             tt(i(8 + j), f(8 + j), f(3), ADD)
         ts(a("sI", 256, 384), a("sI", 256, 384), 4095, AND)
         ts(u(4, 4), a("sI", 256, 384), 16.0, ADD)
-        ts(a("offL"), med("LSp"), -1.0, ADD)
 
         def trial(j):
             tt(a("G4", 512 * j, 512 * j + 512), ind(a("W"), u(4 + j)), a("Zq"), MAX)
-
-        def ga(ch):
-            act(a("GA", 512 + 1024 * ch, 1536 + 1024 * ch), ind(a("drow", 0, 512), a("offL", 64 * ch, 64 * ch + 64)))
 
         act(a("lv", 0, 256), med("LSp"), 1.0, -1.0)
         act(a("lv", 512, 768), med("LSp"), 2.0, 35.0)
         act(a("on16"), med("LSp"), f=AF.Sign)
         act(a("on16"), a("on16"), 8208.0, -8192.0)
-        if t == 1:
-            gather_n("S", 1)
-        ga(0)
         trial(0)
         trial(1)
         if t == 0:
-            consts_b()
             cp(a("rowh", 32, 64), a("gl0"))
             ghost_rows(a("rowh", 32, 64))
         ts(f(16), a("b2", 0, 32), -1.0, ADD, 0.0, MAX)
         cp(u(8), f(16))
         act(a("gr2"), ind(a("drow"), u(8)))
+        if t == 1:
+            ga(0)
         mm(a("b1", 64, 128), a("ID"), a("low", 0, 64), True, False)
         conv(a("b1", 64, 128), "E64", every("G4", 0, 1024), False, True)
         act(a("tA"), a("b1", 64, 128))
         ga(1)
-        ts(f(2), i(2), -1024.0, ADD)
         tt(f(17), a("b3", 0, 32), f(2), ADD)
         ts(f(18), a("b3", 0, 32), 0.0, GT)
         ts(f(26), a("b3", 0, 32), 1.0 / 256, MUL, 508.0, ADD)
-        ts(f(27), i(2), 16.0, MUL)
         conv(a("b3", 32, 64), "Er0", every("gr2", 0, 512))
         trial(2)
         tt(f(17), f(17), a("mneg"), MAX)
@@ -516,7 +498,9 @@ def rank_program(g, core, T, topo):
         mm(a("b2", 64, 128), a("ID"), a("low", 64, 128), True, False)
         conv(a("b2", 64, 128), "E64", every("G4", 1024, 2048), False, True)
         if t == 0:
-            consts_c()
+            act(a("BDdn"), a("BDdp"), -1.0)
+            cp(a("BDo"), a("BDt"))
+            cp(a("offR"), a("rI"))
         mm(a("b4"), a("BDo"), a("prod"), True, False)
         ga(2)
         ga(3)
@@ -540,28 +524,33 @@ def rank_program(g, core, T, topo):
         ts(i(12), i(12), 4095, AND)
         ts(u(14), i(12), 16.0, ADD)
         tt(a("D2", 512, 1024), ind(a("W"), u(14)), a("Zq"), MAX)
-        rows("b5", a("rowh", 0, 32), 32)
-        act(a("dlt"), a("b5"))
+        rows("b7", a("rowh", 0, 32), 32)
+        act(a("dlt"), a("b7"))
         mm(a("b4"), a("BDdp"), a("D2", 512, 1024), False, True)
         act(a("hiT"), a("b4"), cf(6))
+        if t:
+            later[2]()
         if t == 1:
-            for ch in range(2, 6):
-                gather_n("S", ch)
+            gather_n("S", 2)
+            gather_n("S", 3)
             kmax_pe("b5", 0)
+        if t == 0:
+            for n, s, src in (("Ek", cc(5), "E1"), ("Eo", cc(6), "E1"), ("BDo2", cc(6), "BD"), ("En1", cc(3), "E1"), ("En0", cc(23), "E1")):
+                act(a(n), a(src), s)
+            act(a("cB"), a("mA", 0, 16), 1.0, 3840.0)
+            consts_t()
         tt(f(24), f(24), f(18), MUL)
         tt(f(25), a("dA"), f(24), ADD)
         if t < 2:
             cp(a("gs%d" % (t + 1)), f(25))
             send(dn, "gs%d" % (t + 1), "gl%d" % (t + 1), 32, "ag%d" % (t + 1), "lg%d" % (t + 1))
-        ts(a("mk"), med("nrow"), cf(1), EQ)
+        ts(a("mk", 256 * par, 256 * par + 256), med("nrow"), cf(1), EQ)
         tt(a("lvI", 0, 256), a("lv", 0, 256), med("x21"), MUL)
         ts(a("lvI", 0, 256), a("lvI", 0, 256), 4, SHR, 4095, AND)
         cp(ind(a("GA"), u(11)), a("dlt"))
         conv(a("b6", 0, 256), "Er0", every("GA", 512, 4608))
         tt(a("yv"), a("b4"), a("hiT"), SUB)
         cp(ind(a("WK"), u(10)), a("yv"))
-        if t == 0:
-            consts_d()
         mm(a("b7", 0, 256), a("ID"), a("tie"), True, False)
         conv(a("b7", 0, 256), "Ek", every("WK", 512, 4608), False, True)
         tt(a("lv", 256, 512), a("lvI", 0, 256), a("lv", 0, 256), ADD)
@@ -580,14 +569,18 @@ def rank_program(g, core, T, topo):
             scan(a("sc", lo, lo + 1024), a("mask"), a("GL", lo, lo + 1024), 0.0, MAX)
 
         if t == 0:
-            consts_d2()
+            consts_d()
             for ch in range(4):
                 kmax_key("kp", None, ch)
             later[1] = kmax_fin("b1", 224, "km1")
-        elif t == 1:
-            gather_n("S", 6)
-            gather_n("S", 7)
+        if t == 1:
+            gather_n("V", 4)
+            for ch in (5, 6, 7):
+                gather_n("S", ch)
             kmax_key("b5", "C0", 0)
+            kmax_pe("b5", 1)
+        if t:
+            later[3]()
         cp(a("tk", 64, 192), a("b7", 128, 256))
         tt(a("tk", 192, 320), a("b7", 0, 128), a("tk", 64, 192), MAX)
         tt(a("tk", 320, 384), a("tk", 192, 256), a("tk", 256, 320), MAX)
@@ -602,7 +595,7 @@ def rank_program(g, core, T, topo):
         conv(a("b1", 128, 144), "Eo", every("wr", 0, 256))
         mm(a("b4", 0, 256), a("BDo2"), a("wr"), True, True)
         if t < 2:
-            mm(a("b3", 128, 144), a("ONE"), a("sBb", 0, 16), True, True)
+            mm(a("b3", 128, 144), a("ones", 0, 128), a("sBb", 0, 16), True, True)
         level_scan(0)
         tt(a("sB", 32, 48), a("b1", 128, 144), a("sB", 16, 32), MUL)
         ts(a("sBb", 16, 32), a("sB", 32, 48), 512.5, GT)
@@ -611,10 +604,8 @@ def rank_program(g, core, T, topo):
         tt(a("eqo"), med("LSp"), a("b4", 0, 256), EQ)
         mm(a("b1", 192, 208), a("ID"), a("full"), True, False)
         conv(a("b1", 192, 208), "E1", every("eqo", 0, 256), False, True)
-        if t == 1:
-            kmax_pe("b5", 1)
         ts(a("sB", 48, 64), a("sB", 32, 48), -512.0, ADD, 0.0, MAX)
-        scan(a("sB", 64, 80), a("ONE", 0, 16), a("b2", 128, 144), -60.0, ADD)
+        scan(a("sB", 64, 80), a("ones", 0, 16), a("b2", 128, 144), -60.0, ADD)
         tt(a("sB", 80, 96), a("sB", 64, 80), a("b2", 144, 160), LE)
         tt(a("sB", 96, 112), a("sB", 80, 96), a("sB", 48, 64), MUL)
         ts(a("kwI", 0, 16), a("sB", 96, 112), -1.0, ADD)
@@ -630,16 +621,28 @@ def rank_program(g, core, T, topo):
         send(up, "hs%d" % t, "hl%d" % t, 32, "ah%d" % t, "lh%d" % t)
         tt(a("sB", 144, 160), a("sB", 144, 160), a("b1", 192, 208), GT)
         tt(a("jv"), a("sB", 144, 160), a("sB", 32, 48), MUL)
+        cp(a("jw", 0, 16), a("jv"))
+        tt(a("jw", 16, 32), a("jv"), a("jw", 0, 16), SUB)
         if t == 0:
             consts_e()
         if t < 2:
             for h in range(2):
                 k = 128 * (2 * par + h)
                 mm(a("b3", 160 + h, 192, 2), a("HX", k, k + 128), a("jv"), True, True)
+
+        def jv_rows():
+            rows("b2", a("jw", 0, 16), 16, 256, a("jw", 16, 32))
+
+        if t == 2:
+            jv_rows()
         if t == 1:
             kmax_key("b5", "C0", 1)
             kmax_pe("b5", 2)
         level_scan(1)
+        if t == 0:
+            ts(a("jw", 32, 48), a("jv"), 1.0, MIN)
+            rows("b2", a("jw", 32, 48), 16, 256)
+            act(a("sg"), a("b2", 256, 512))
         if t < 2:
             if t == 0:
                 cp(a("oX"), a("b3", 160, 192))
@@ -657,54 +660,50 @@ def rank_program(g, core, T, topo):
         mm(a("b6", 256, 512), a("ID"), a("sc", 15, 4096, 16), False, True)
         if t == 1:
             kmax_key("b5", "C0", 2)
-        ts(a("zI"), a("b6", 256, 512), 0.5, MUL, -0.25, ADD)
-        cp(a("zs"), a("zI"))
+            kmax_pe("b5", 3)
+        act(a("zf"), a("b6", 256, 512), 0.5, -0.25)
+        act(a("zf"), a("zf"), 1.0, 12582912.0)
+        act(a("zs"), a("zf"), 1.0, -12582912.0)
         send((rank + 1 + t) % N, "zs", "z%d" % (t + 1), 256, "az%d" % t, "lz%d" % t)
 
         def lists(t=t, med=med):
-            tt(a("lv", 1024, 1280), a("b2", 256, 512), a("mk"), MUL)
+            tt(a("lv", 1024, 1280), a("b2", 256, 512), a("mk", 256 * (t & 1), 256 * (t & 1) + 256), MUL)
             tt(med("LSp"), med("LSp"), a("lv", 1024, 1280), ADD)
             if t == 0:
-                ts(a("lv", 1024, 1280), a("b2", 256, 512), 0.5, GT)
-                tt(a("nrow", 0, 512, 2), a("nrow", 0, 512, 2), a("lv", 1024, 1280), ADD)
-                ts(a("T01", 1, 513, 2), a("nrow", 0, 512, 2), cc(8), MUL, cc(9), ADD)
-            if t < 2:
-                emit("V", a("sB", 160, 161), [a("b3", 128, 144)], lambda e: e.tensor_reduce(a("sB", 160, 161)[0], a("b3", 128, 144)[0], axis=AxisListType.X, op=ADD))
-                cp(a("kwI", 0, 1), a("sB", 160, 161))
-                ts(a("kwI", 1, 2), a("kwI", 0, 1), 31, AND)
-                cp(a("sB", 161, 162), a("kwI", 1, 2))
-                ts(a("thT"), a("thB"), a("sB", 161, 162), ADD, 4080.0, MIN)
-                ts(a("thK"), a("thT"), 4096.0, MUL, 4095.0, ADD)
+                tt(a("nrow", 0, 512, 2), a("nrow", 0, 512, 2), a("sg"), ADD)
+
+        def limits():
+            emit("V", a("sB", 160, 161), [a("b3", 128, 144)], lambda e: e.tensor_reduce(a("sB", 160, 161)[0], a("b3", 128, 144)[0], axis=AxisListType.X, op=ADD))
+            cp(a("kwI", 0, 1), a("sB", 160, 161))
+            ts(a("kwI", 1, 2), a("kwI", 0, 1), 31, AND)
+            cp(a("sB", 161, 162), a("kwI", 1, 2))
+            ts(a("thT"), a("thB"), a("sB", 161, 162), ADD, 4080.0, MIN)
+            ts(a("thK"), a("thT"), 4096.0, MUL, 4095.0, ADD)
 
         if t < 2:
-            later[0] = lists
             conv(a("b3", 192, 224), "En1" if t == 0 else "En0", every("gr", 0, 512))
             iota(a("WK", 512), [[0, 4096]], 0, 0)
-        else:
-            rows("b2", a("jv"), 16, 256)
-            lists()
-            ts(a("ky"), a("LSp", 0, 512), -1.0, ADD)
-            dma("D", T.yl[:, :], a("ky")[0], [(("ky", 0, 512), False)])
         tt(i(13), f(25), a("hl%d" % t), ADD)
         ts(i(14), i(13), 15, AND)
         cp(a("rowh", 0, 32), i(14))
         rows("b4", a("rowh", 0, 32), 32)
+        if t == 0:
+            tt(a("T01", 1, 513, 2), a("T01", 1, 513, 2), a("sg"), ADD)
+            gather_n("S", 0)
+        elif t == 1:
+            kmax_key("b5", "C0", 3)
+            later[1] = kmax_fin("b1", 224, "km2")
         if t < 2:
             tt(f(31), f(30), a("b3", 192, 224), ADD)
-            if t == 0:
-                later[1]()
+            later[1]()
             act(a("drow", 0, 512), a("b4"))
-            if t == 1:
-                kmax_pe("b5", 3)
             cp(a("dA"), i(14))
             trial_tables()
-            if t == 1:
-                kmax_key("b5", "C0", 3)
-                km2 = kmax_fin("b1", 224, "km2")
-            rows("b2", a("jv"), 16, 256)
-            if t == 1:
-                km2()
+            later[0], later[2], later[3] = limits, jv_rows, lists
         else:
+            lists()
+            ts(a("ky"), a("LSp", 0, 512), -1.0, ADD)
+            dma("D", T.yl[:, :], a("ky")[0], [(("ky", 0, 512), False)])
             act(a("kyT"), a("b4"))
             dma("D", T.yd[:, :], T.kyT[0:128:16, :], [(("kyT", 0, 512), False)])
             dma("D", T.yz[:, :], T.z3[:, :], [(("z3", 0, 256), False)])

from concourse.mybir import AluOpType, ActivationFunctionType, AxisListType

F, B, H, I, U = "float32", "bfloat16", "float16", "int32", "uint16"
SB = {
    "X": (512, F), "gx": (128, F), "mA": (32, F), "ci": (16, I), "cf": (16, F), "cc": (32, F),
    "BD": (128, B), "BDh": (128, H), "BDdp": (128, B), "BDdn": (128, B), "BDo": (128, H), "BDo2": (128, B), "BDt": (128, B),
    "ID": (128, B), "TRI": (128, B), "ones": (2048, B), "Tlo": (128, B), "x32": (512, B), "rI": (32, I), "offR": (32, U), "FH": (2048, B),
    "E64": (144, B), "Er0": (144, B), "En0": (144, B), "En1": (144, B), "En2": (144, B), "Es": (144, B), "Ek": (144, B), "Eo": (144, B),
    "E1": (144, B), "Eth": (144, B), "Eh": (144, H),
    "TA": (1024, H), "HX": (512, H), "mask": (1024, B), "tie": (256, B), "Mrow": (512, F), "x21": (512, F), "x613": (512, F),
    "m21": (32, F), "m37": (32, F), "m613": (32, F), "mneg": (32, F), "cB": (16, F),
    "glI": (512, I), "LSp": (528, F), "offN": (512, U), "onb": (512, B), "C": (512, F), "C0": (512, F), "C1": (512, F), "GN": (8192, B), "T01": (528, B),
    "nrow": (512, B), "ky": (512, F), "kyT": (512, F), "ks": (512, F), "kp": (512, F), "kI": (32, I), "khI": (32, I), "khH": (32, H), "klI": (32, I), "klH": (32, H),
    "km0": (32, F), "km1": (32, F), "km2": (32, F), "c15m": (32, F),
    "W": (4112, B), "nbI": (512, I), "vr0": (512, I), "vrh": (512, H), "thr": (256, I), "thI": (512, I), "thb": (512, B), "thB": (16, F), "thK": (16, F), "thT": (16, F),
    "z0": (272, B), "z1": (272, B), "z2": (272, B), "z3": (256, B), "drow": (1024, B),
    "dA": (32, F), "p4": (128, F), "pI": (256, I), "low": (128, B),
    "gs0": (32, B), "gs1": (32, B), "gs2": (32, B), "gl0": (32, B), "gl1": (32, B), "gl2": (32, B),
    "hs0": (32, B), "hs1": (32, B), "hs2": (32, B), "hl0": (32, B), "hl1": (32, B), "hl2": (32, B),
    "sI": (512, I), "sF": (1024, F), "sU": (512, U), "eq": (512, B), "Zq": (512, B), "gr": (512, B), "gr2": (512, B), "prod": (512, H),
    "G4": (2048, B), "D2": (1024, B), "tA": (64, F), "rowh": (64, B), "dlt": (512, B), "WK": (4608, B),
    "GA": (4608, B), "GL": (4096, B), "sc": (4096, B), "offL": (256, U), "offM": (256, U), "zs": (256, B), "zf": (256, F), "lv": (1280, F), "lvI": (512, I),
    "on16": (256, F), "hiT": (512, B), "yv": (512, B), "tk": (512, F), "kwI": (32, I), "wr": (256, B), "eqo": (256, B), "sg": (256, B),
    "sB": (256, F), "sBb": (64, B), "full": (16, B), "mk": (512, B), "jv": (16, H), "jw": (48, B), "oX": (32, F), "lt": (2048, B), "rt": (512, B),
}
ALIAS = {}


def share(to, names):
    at = 0
    for n in names:
        ALIAS[n] = (to, at)
        at += SB[n][0]
    return at


SCRATCH = {}
for _to, _ns in (("aI", ("vr0", "nbI", "thr", "thI")), ("aB", ("onb", "thb")), ("aF", ("ks", "kp")),
                 ("sm", ("m21", "m37", "m613", "mneg", "c15m", "km0", "km1", "km2", "oX", "dA", "tA", "cB", "thB", "thK", "thT")),
                 ("smI", ("kI", "khI", "klI", "rI", "kwI")),
                 ("EE", ("E64", "Er0", "En0", "En1", "En2", "Es", "Ek", "Eo", "E1", "Eth"))):
    SCRATCH[_to] = ("sbuf", [128, share(_to, _ns)], SB[_ns[0]][1])
for _n in SB:
    if _n not in ALIAS:
        SCRATCH[_n] = ("sbuf", [128, SB[_n][0]], SB[_n][1])
for _b in range(8):
    SCRATCH["b%d" % _b] = ("psum", [128, 512], F)
SEMAPHORES = ["sV", "sS", "sP", "sG"] + ["d%d" % i for i in range(12)] + [a + str(t) for a in ("az", "ah", "ag", "lz", "lh", "lg") for t in range(3)]


def rank_program(g, core, T, topo):
    rank = T.rank_of(core)
    if rank is None:
        return
    N = len(T.cores)
    OP, AF = AluOpType, ActivationFunctionType
    ADD, SUB, MUL, MAX, MIN = OP.add, OP.subtract, OP.mult, OP.max, OP.min
    GT, GE, LT, LE, EQ = OP.is_gt, OP.is_ge, OP.is_lt, OP.is_le, OP.is_equal
    SHR, AND = OP.arith_shift_right, OP.bitwise_and
    eng = {"V": g.vector, "S": g.scalar, "P": g.tensor, "G": g, "D": g.sync}
    hist, known, total, nd = {}, {q: {} for q in "VSPGD"}, {}, [0]
    banks = ["b%d" % k for k in range(8)]

    def order(q, acc):
        toks = []
        for (n, lo, hi), w in acc:
            for r in hist.get(n, []):
                if n in banks and r[3] != q:
                    toks.append(r[4])
                    continue
                if not (lo < r[1] and r[0] < hi) or not (w or r[2]):
                    continue
                if r[3] == q == "P":
                    continue
                toks.append(r[4])
        toks.sort(key=lambda k: -len(k[2]))
        for i, (s, v, kn) in enumerate(toks):
            if known[q].get(s, 0) >= v:
                continue
            if any(j != i and (k[2].get(s, 0) >= v and (k[0] != s or k[1] > v)) for j, k in enumerate(toks)):
                continue
            eng[q].wait_ge(T.sem[s], v)
            for a, b in kn.items():
                known[q][a] = max(known[q].get(a, 0), b)
            known[q][s] = max(known[q].get(s, 0), v)

    def note(q, acc, tok, dma=False):
        for (n, lo, hi), w in acc:
            keep = []
            for r in hist.get(n, []):
                inside = lo <= r[0] and r[1] <= hi
                ps = n in banks
                if inside and (w if not ps else (w or not r[2])) and not (ps and r[3] != q and not w):
                    continue
                if inside and not w and not r[2] and r[3] == q and not dma:
                    continue
                keep.append(r)
            keep.append((lo, hi, w, "dma" if dma else q, tok))
            hist[n] = keep

    def emit(q, outs, ins, call):
        acc = [(a, False) for v in ins if v is not None and not isinstance(v, (int, float)) for a in v[1]] + [(a, True) for a in outs[1]]
        order(q, acc)
        s = "s" + q
        total[s] = total.get(s, 0) + 1
        call(eng[q]).then_inc(T.sem[s], 1)
        kn = dict(known[q])
        kn[s] = total[s]
        note(q, acc, (s, total[s], kn))

    def a(n, lo=0, hi=None, st=1):
        hi = SB[n][0] if hi is None and n in SB else 512 if hi is None else hi
        if n in ALIAS:
            o = ALIAS[n][1]
            n, lo, hi = ALIAS[n][0], lo + o, hi + o
        return (T[n][:, lo:hi:st] if st > 1 else T[n][:, lo:hi], [(n, lo, hi)])

    def ind(w, o):
        return (w[0].indirect(o[0]), w[1] + o[1])

    def x(v):
        return v if v is None or isinstance(v, (int, float)) else v[0]

    def ts(o, i, s1, op0, s2=None, op1=None):
        if op1 is None:
            emit("V", o, [i, s1], lambda e: e.tensor_scalar(o[0], i[0], x(s1), None, op0))
        else:
            emit("V", o, [i, s1, s2], lambda e: e.tensor_scalar(o[0], i[0], x(s1), x(s2), op0, op1))

    def tt(o, i, j, op):
        emit("V", o, [i, j], lambda e: e.tensor_tensor(o[0], i[0], j[0], op))

    def cp(o, i):
        emit("V", o, [i], lambda e: e.tensor_copy(o[0], i[0]))

    def fill(o, c):
        emit("V", o, [], lambda e: e.memset(o[0], c))

    def scan(o, d0, d1, init, op1):
        emit("V", o, [d0, d1], lambda e: e.tensor_tensor_scan(o[0], d0[0], d1[0], init, MUL, op1))

    def act(o, i, scale=1.0, bias=0.0, f=None):
        f = (AF.Copy if bias == 0.0 else AF.Identity) if f is None else f
        emit("S", o, [i, scale], lambda e: e.activation(o[0], i[0], f, bias=bias, scale=x(scale)))

    def mm(o, l, r, start, stop):
        emit("P", o, [l, r], lambda e: e.matmul(o[0], l[0], r[0], start, stop))

    def iota(o, pat, base, cm):
        emit("G", o, [], lambda e: e.iota(o[0], pat, base, cm, allow_small_or_imprecise_dtypes=True))

    def keep(o, i, pat, op, base, cm, c=0.0):
        emit("G", o, [i], lambda e: e.affine_select(o[0], i[0], pat, op, c, base, cm))

    def dma(q, out, in_, acc):
        order(q, acc)
        s = "d%d" % nd[0]
        nd[0] += 1
        eng[q].dma_start(out, in_).then_inc(T.sem[s], 16)
        total[s] = 16
        kn = dict(known[q])
        kn[s] = 16
        note(q, acc, (s, 16, kn), True)

    def es(E, q):
        return a(E, 15 - q, 143 - q)

    def conv(o, E, src, first=True, last=True):
        for q in range(16):
            mm(o, es(E, q), src(q), first and q == 0, last and q == 15)

    def every(n, lo, hi):
        return lambda q: a(n, lo + q, hi, 16)

    def rows(bank, src, n, lo=0, rest=None):
        for q in range(16):
            o, w = a(bank, lo + q, lo + 16 * n, 16), a("FH", 128 * q, 128 * q + 128)
            mm(o, w, src, True, rest is None)
            if rest is not None:
                mm(o, w, rest, False, True)

    def send(dst, buf, rbuf, n, arr, loc):
        to = T.cores[dst]
        use = topo.engines(core, to)[:8]
        rid, pid = topo.addr(to)[0], topo.addr(to)[1]
        acc = [((buf, 0, n), False)]
        order("G", acc)
        g.remote_dma(T[rbuf][:, 0:n], T[buf][:, 0:n], T.sem[arr], T.sem[loc], pid, rid, sum(1 << e for e in use))
        total[loc] = len(use)
        note("G", acc, (loc, len(use), {loc: len(use)}), True)

    def lands(src, buf, n, arr):
        k = len(topo.engines(T.cores[src], core)[:8])
        total[arr] = k
        note("R", [((buf, 0, n), True)], (arr, k, {arr: k}), True)

    up, dn = (rank + 1) % N, (rank - 1) % N
    for t in range(3):
        lands((rank - 1 - t) % N, "z%d" % (t + 1), 256, "az%d" % t)
        lands(dn, "hl%d" % t, 32, "ah%d" % t)
        lands(up, "gl%d" % t, 32, "ag%d" % t)

    def load(q, v, src, part=None):
        dma(q, v[0] if part is None else part, src, [(r, True) for r in v[1]])

    load("D", a("glI"), T.gl[:, :])
    iota(a("ci", 0, 1), [[0, 1]], 0, 1)
    iota(a("gx"), [[1, 8], [0, 16]], 0, 0)
    iota(a("X"), [[1, 512]], 0, 0)
    load("S", a("W", 16), T.rec[:, :])
    fill(a("vr0"), 0)
    fill(a("thr"), 0)
    load("D", a("vr0"), T.val[:, :], T["aI"][0:128:16, 0:512])
    load("D", a("nbI"), T.nb[:, :])
    load("D", a("z0", 0, 256), T.zl[:, :])
    load("D", a("thr"), T.th[:, :], T["aI"][0:128:16, 1024:1280])
    iota(a("ones"), [[0, 2048]], 1, 0)
    keep(a("mask"), a("ones", 0, 1024), [[0, 64], [1, 16]], GT, 0, 0)
    iota(a("mA"), [[16, 32]], 0, 1)
    iota(a("tie"), [[-256, 16], [0, 16]], 3840, 0)
    iota(a("x32"), [[0, 16], [1, 32]], 0, 0)
    iota(a("rI"), [[1, 16], [0, 2]], 0, 0)
    keep(a("ID"), a("ones", 0, 128), [[-1, 128]], EQ, 0, 1)
    keep(a("FH"), a("ones"), [[-1, 16], [-16, 8], [0, 16]], EQ, 0, 1)
    iota(a("Tlo"), [[0, 8], [1, 16]], 0, 0)
    keep(a("Tlo"), a("Tlo"), [[-16, 8], [0, 16]], GE, 0, 1, -1.0)
    keep(a("Tlo"), a("Tlo"), [[16, 8], [0, 16]], GE, 15, -1, -1.0)

    for n, (op, c) in enumerate(((AND, 15), (AND, 112), (AND, 96), (SHR, 4), (AND, 14), (AND, 1), (AND, 7), (AND, 8))):
        ts(a("ci", n + 1, n + 2), a("ci", 0, 1), c, op)
    ts(a("ci", 9, 10), a("ci", 0, 1), 4, SHR, 1, AND)
    cp(a("cf", 0, 10), a("ci", 0, 10))

    def cf(n):
        return a("cf", n, n + 1)

    def cc(n):
        return a("cc", n, n + 1)

    def mk_e(n, w):
        ts(a(n), a("X", 0, 144), cc(0), EQ, w, MUL)

    ts(a("BD"), a("gx"), cf(4), EQ)
    keep(a("BDdp"), a("BD"), [[0, 8], [-1, 16]], GE, 1, 0)
    keep(a("BDt"), a("BD"), [[0, 8], [1, 16]], GE, -2, 0)
    keep(a("BDt"), a("BDt"), [[0, 8], [-1, 16]], GE, 3, 0)
    keep(a("TRI"), a("BD"), [[-1, 128]], GT, 0, 1)
    ts(cc(8), cf(1), 1.0, OP.not_equal)
    ts(cc(7), cf(1), 0.0, OP.not_equal)
    ts(cc(9), cc(8), 33.0, MUL, -32.0, ADD)
    ts(cc(10), cc(7), 33.0, MUL, -32.0, ADD)
    ts(cc(0), cf(2), 15.0, ADD)
    ts(cc(2), cf(1), 2.0, EQ, 16384.0, MUL)
    ts(cc(11), cf(1), -1024.0, MUL, 15359.0, ADD)
    fill(a("T01", 0, 1), -32.0)
    mk_e("En2", cc(2))
    ts(a("LSp", 0, 512), a("glI"), 1.0, ADD)
    act(a("onb"), a("LSp", 0, 512), f=AF.Sign)
    ts(a("offN"), a("glI"), 1.0, ADD)
    mm(a("b5"), a("BD"), a("onb"), True, True)
    ts(a("T01", 1, 513, 2), a("b5", 0, 512, 2), cc(8), MUL, cc(9), ADD)
    ts(a("T01", 2, 514, 2), a("b5", 1, 512, 2), cc(7), MUL, cc(10), ADD)

    def gather_n(q, ch):
        o, i = a("GN", 1024 * ch, 1024 * ch + 1024), ind(a("T01", 0, 513), a("offN", 64 * ch, 64 * ch + 64))
        if q == "V":
            cp(o, i)
        else:
            act(o, i)

    def kmax_pe(bank, ch):
        conv(a(bank, 128 * ch, 128 * ch + 128), "En2", every("GN", 2048 * ch, 2048 * ch + 2048))

    def kmax_key(src, add, ch):
        lo, hi = 128 * ch, 128 * ch + 128
        if add is not None:
            tt(a("ky", lo, hi), a(src, lo, hi), a(add, lo, hi), ADD)
            src = "ky"
        emit("V", a("kyT", lo, hi), [a(src, lo, hi)], lambda e: e.transpose(a("kyT", lo, hi)[0], a(src, lo, hi)[0]))
        scan(a("ks", lo, hi), a("mask", 0, 128), a("kyT", lo, hi), 0.0, MAX)

    def kmax_fin(small, so, dest):
        cp(a("kI"), a("ks", 15, 512, 16))
        ts(a("khI"), a("kI"), 10, SHR)
        ts(a("klI"), a("kI"), 1023, AND)
        cp(a("khH"), a("khI"))
        cp(a("klH"), a("klI"))
        for c1 in range(2):
            n = 0
            for g1 in range(2):
                for part, src in ((1, "khH"), (0, "klH")):
                    k = 128 * (4 * part + 2 * c1 + g1)
                    mm(a(small, so + c1, so + 32, 2), a("TA", k, k + 128), a(src, g1, 32, 2), n == 0, n == 3)
                    n += 1
        return lambda: ts(a(dest), a(small, so, so + 32), 512.0, MAX)

    for ch in range(1, 6):
        gather_n("S", ch)
    for ch in (0, 6, 7):
        gather_n("V", ch)
    ts(a("mA"), a("mA"), cf(2), SUB)
    mk_e("E1", 1.0)
    kmax_pe("b6", 0)
    kmax_pe("b6", 1)
    kmax_pe("b4", 3)
    kmax_pe("b4", 2)
    ts(a("C"), a("LSp", 0, 512), cc(11), ADD)
    ts(a("lvI", 0, 512), a("glI"), 1, AND)
    ts(a("kp"), a("lvI", 0, 512), -524288.0, MUL)
    tt(a("C0"), a("C"), a("kp"), ADD)
    kmax_key("b6", "C0", 0)
    kmax_key("b6", "C0", 1)
    mk_e("Eh", 1.0)
    cp(a("BDh"), a("BD"))
    cp(a("vrh"), a("vr0"))
    mm(a("b7"), a("BDh"), a("vrh"), True, True)
    conv(a("b3", 0, 32), "Eh", every("vrh", 0, 512))
    for n, s, b, src in (("m21", 2.0, 1.0, "mA"), ("m37", 2.0, 37.0, "mA"), ("m613", 2.0, 613.0, "mA"), ("mneg", 1.0, -512.0, "mA"),
                         ("Mrow", 1.0, 1.0, "X"), ("x613", 2.0, 613.0, "X"), ("x21", 2.0, 1.0, "X")):
        act(a(n), a(src), s, b)
    act(a("nrow"), a("b5"))
    act(a("drow", 0, 512), a("b7"))
    act(a("C1"), a("kp"), -2.0, -524288.0)
    for g1 in range(2):
        ts(cc(16 + g1), cf(3), cf(1), ADD, 16.0 * g1, ADD)
    ts(cc(18), cf(9), 0.0, EQ)
    for c1, c in enumerate((cc(18), cf(9))):
        ts(cc(20 + c1), c, 1024.0, MUL)
        for g1 in range(2):
            for part in range(2):
                k = 128 * (4 * part + 2 * c1 + g1)
                ts(a("TA", k, k + 128), a("X", 0, 128), cc(16 + g1), EQ, cc(20 + c1) if part else c, MUL)
    kmax_key("b4", "C0", 3)
    kmax_key("b4", "C0", 2)
    km0 = kmax_fin("b1", 0, "km0")
    ts(cc(1), cf(1), 0.0, EQ)
    ts(cc(4), cf(1), 256.0, MUL, 1024.0, ADD)
    ts(cc(5), cf(5), 0.0, EQ, 4096.0, MUL)
    ts(cc(6), cf(5), 2.0, EQ)
    ts(cc(22), cc(1), 64.0, MUL)
    ts(cc(3), cf(1), 1.0, EQ, 16384.0, MUL)
    ts(cc(23), cc(1), 16384.0, MUL)
    act(a("Er0"), a("E1"), cc(1))
    km0()
    cp(a("dA"), a("b3", 0, 32))
    cp(a("gs0"), a("dA"))
    send(dn, "gs0", "gl0", 32, "ag0", "lg0")
    iota(a("WK", 512), [[0, 4096]], 0, 0)
    later = [None] * 4
    fill(a("LSp", 512, 528), 0.0)
    fill(a("drow", 512, 528), 0.0)
    fill(a("W", 0, 16), 0.0)
    fill(a("z0", 256, 272), 0.0)

    def trial_tables():
        for j in range(4):
            ts(a("pI", 32 * j, 32 * j + 32), a("dA"), float(j), ADD)
        ts(a("pI", 128, 256), a("pI", 0, 128), 15, AND)
        cp(a("p4"), a("pI", 128, 256))

    def consts_t():
        ts(a("thI", 0, 256), a("thr"), 6, SHR)
        ts(a("thI", 256, 512), a("thr"), 63, AND)
        cp(a("thb"), a("thI"))
        conv(a("b5", 64, 80), "Eth", every("thb", 0, 256), True, False)
        conv(a("b5", 64, 80), "Er0", every("thb", 256, 512), False, True)
        conv(a("b5", 96, 128), "Er0", every("nrow", 0, 512))

    def consts_d():
        cp(a("thB"), a("b5", 64, 80))
        ts(a("thK"), a("thB"), 4096.0, MUL, 4095.0, ADD)
        ts(a("c15m"), a("b5", 96, 128), -1024.0, MUL, 15359.0, ADD)

    def consts_e():
        ts(cc(12), cf(7), 2.0, MUL, cf(2), ADD)
        ts(cc(13), cc(12), 1.0, ADD)
        ts(cc(14), cf(8), 0.0, EQ)
        ts(cc(15), cf(8), 0.0, GT)
        for t in range(2):
            for h in range(2):
                k = 128 * (2 * t + h)
                ts(a("HX", k, k + 128), a("X", 0, 128), cc(12 + t), EQ, cc(14 + h), MUL)
        for t in (1, 2):
            fill(a("z%d" % t, 256, 272), 0.0)

    def ghost_rows(src):
        rows("b7", src, 32)
        act(a("drow", 512, 1024), a("b7"))

    def f(n):
        return a("sF", 32 * n, 32 * n + 32)

    def i(n):
        return a("sI", 32 * n, 32 * n + 32)

    def u(n, m=1):
        return a("sU", 32 * n, 32 * (n + m))

    for t in range(3):
        par, zt = t & 1, "z%d" % t

        def med(n, o=0, par=par):
            return a(n, o + par, o + 512, 2)

        if t == 0:
            cp(i(0), a("km0"))
        else:
            tt(i(0), a("km%d" % t), f(31), MAX)
        ts(i(1), i(0), 1023, AND)
        cp(u(0), i(1))
        ts(i(2), i(0), 1, SHR, 511, AND)
        cp(u(2), i(2))
        act(a("gr"), ind(a("drow", 0, 528), u(0)))
        ts(f(0), i(1), 2.0, MUL, 1.0, ADD)
        ts(a("offL"), med("LSp"), -1.0, ADD)
        tt(a("eq"), ind(a("LSp"), u(0)), a("Mrow"), EQ)
        if t == 0:
            act(a("Zq"), ind(a(zt), u(2)))

        def ga(ch):
            act(a("GA", 512 + 1024 * ch, 1536 + 1024 * ch), ind(a("drow", 0, 512), a("offL", 64 * ch, 64 * ch + 64)))

        if t == 0:
            for n, c in (("Es", cc(4)), ("E64", 64.0), ("Eth", cc(22))):
                act(a(n), a("E1"), c)
            trial_tables()
        for j in range(4):
            act(f(4 + j), f(0), 1.0, 612.0)
        act(f(2), f(0), 0.25, -1024.25 - 0.5 * par)
        act(f(27), f(0), 4.0, -4.0 - 8.0 * par)
        for j in range(4):
            act(a("low", 32 * j, 32 * j + 32), a("p4", 32 * j, 32 * j + 32), 1.0, 16.0 * j)
        if t:
            act(a("Zq"), ind(a(zt), u(2)))
        if t != 1:
            ga(0)
        else:
            gather_n("S", 1)
        if t:
            later[0]()
        conv(a("b1", 0, 32), "Er0", every("gr", 0, 512))
        conv(a("b3", 0, 32), "Es", every("eq", 0, 512))
        tt(i(3), f(0), a("mA"), MUL)
        ts(i(4), i(3), 4, SHR, 4095, AND)
        tt(f(1), i(4), a("mA"), ADD)
        tt(a("sF", 256, 384), a("p4"), a("sF", 128, 256), MUL)
        if t == 0:
            tt(a("kp"), a("ky"), a("C1"), ADD)
            ts(a("b0"), a("nbI"), 1.0, ADD)
        tt(a("prod"), a("b0"), a("eq"), MUL)
        conv(a("b2", 0, 32), "Eh", every("prod", 0, 512))
        if t:
            ghost_rows(a("rowh", 32, 64))
        conv(a("b4", 0, 16), "Er0", lambda q: a("nrow", 2 * q + par, 512, 32))
        tt(f(3), a("b1", 0, 32), a("m37"), MUL)
        tt(f(3), f(3), f(1), ADD)
        for j in range(4):
            tt(i(8 + j), f(8 + j), f(3), ADD)
        ts(a("sI", 256, 384), a("sI", 256, 384), 4095, AND)
        ts(u(4, 4), a("sI", 256, 384), 16.0, ADD)

        def trial(j):
            tt(a("G4", 512 * j, 512 * j + 512), ind(a("W"), u(4 + j)), a("Zq"), MAX)

        act(a("lv", 0, 256), med("LSp"), 1.0, -1.0)
        act(a("lv", 512, 768), med("LSp"), 2.0, 35.0)
        act(a("on16"), med("LSp"), f=AF.Sign)
        act(a("on16"), a("on16"), 8208.0, -8192.0)
        trial(0)
        trial(1)
        if t == 0:
            cp(a("rowh", 32, 64), a("gl0"))
            ghost_rows(a("rowh", 32, 64))
        ts(f(16), a("b2", 0, 32), -1.0, ADD, 0.0, MAX)
        cp(u(8), f(16))
        act(a("gr2"), ind(a("drow"), u(8)))
        if t == 1:
            ga(0)
        mm(a("b1", 64, 128), a("ID"), a("low", 0, 64), True, False)
        conv(a("b1", 64, 128), "E64", every("G4", 0, 1024), False, True)
        act(a("tA"), a("b1", 64, 128))
        ga(1)
        tt(f(17), a("b3", 0, 32), f(2), ADD)
        ts(f(18), a("b3", 0, 32), 0.0, GT)
        ts(f(26), a("b3", 0, 32), 1.0 / 256, MUL, 508.0, ADD)
        conv(a("b3", 32, 64), "Er0", every("gr2", 0, 512))
        trial(2)
        tt(f(17), f(17), a("mneg"), MAX)
        tt(i(5), f(16), a("m21"), MUL)
        ts(f(20), f(16), 2.0, MUL, 37.0, ADD)
        ts(u(10), f(17), 512.0, ADD)
        ts(i(5), i(5), 4, SHR, 4095, AND)
        tt(f(22), a("dA"), f(20), MUL)
        tt(f(26), f(26), f(27), ADD)
        ts(a("full"), a("b4", 0, 16), 15.5, GT)
        tt(f(26), f(26), f(18), MUL)
        trial(3)
        mm(a("b2", 64, 128), a("ID"), a("low", 64, 128), True, False)
        conv(a("b2", 64, 128), "E64", every("G4", 1024, 2048), False, True)
        if t == 0:
            act(a("BDdn"), a("BDdp"), -1.0)
            cp(a("BDo"), a("BDt"))
            cp(a("offR"), a("rI"))
        mm(a("b4"), a("BDo"), a("prod"), True, False)
        ga(2)
        ga(3)
        tt(f(26), f(26), a("mA"), MAX)
        tt(f(19), i(5), f(16), ADD)
        cp(u(11), f(26))
        tt(f(21), a("b3", 32, 64), a("m613"), MUL)
        tt(f(19), f(19), f(21), ADD)
        tt(i(6), f(22), f(19), ADD)
        ts(i(6), i(6), 4095, AND)
        ts(u(12), i(6), 16.0, ADD)
        tt(a("D2", 0, 512), ind(a("W"), u(12)), a("Zq"), MAX)
        mm(a("b4"), a("BDdn"), a("D2", 0, 512), False, False)
        tt(a("tk", 0, 64), a("tA"), a("b2", 64, 128), MIN)
        tt(i(7), a("tk", 0, 32), a("tk", 32, 64), MIN)
        ts(i(7), i(7), 15, AND)
        tt(f(23), i(7), f(20), MUL)
        cp(a("rowh", 0, 32), i(7))
        tt(i(12), f(23), f(19), ADD)
        tt(f(24), i(7), a("dA"), SUB)
        ts(i(12), i(12), 4095, AND)
        ts(u(14), i(12), 16.0, ADD)
        tt(a("D2", 512, 1024), ind(a("W"), u(14)), a("Zq"), MAX)
        rows("b7", a("rowh", 0, 32), 32)
        act(a("dlt"), a("b7"))
        mm(a("b4"), a("BDdp"), a("D2", 512, 1024), False, True)
        act(a("hiT"), a("b4"), cf(6))
        if t:
            later[2]()
        if t == 1:
            gather_n("S", 2)
            gather_n("S", 3)
            kmax_pe("b5", 0)
        if t == 0:
            for n, s, src in (("Ek", cc(5), "E1"), ("Eo", cc(6), "E1"), ("BDo2", cc(6), "BD"), ("En1", cc(3), "E1"), ("En0", cc(23), "E1")):
                act(a(n), a(src), s)
            act(a("cB"), a("mA", 0, 16), 1.0, 3840.0)
            consts_t()
        tt(f(24), f(24), f(18), MUL)
        tt(f(25), a("dA"), f(24), ADD)
        if t < 2:
            cp(a("gs%d" % (t + 1)), f(25))
            send(dn, "gs%d" % (t + 1), "gl%d" % (t + 1), 32, "ag%d" % (t + 1), "lg%d" % (t + 1))
        ts(a("mk", 256 * par, 256 * par + 256), med("nrow"), cf(1), EQ)
        tt(a("lvI", 0, 256), a("lv", 0, 256), med("x21"), MUL)
        ts(a("lvI", 0, 256), a("lvI", 0, 256), 4, SHR, 4095, AND)
        cp(ind(a("GA"), u(11)), a("dlt"))
        conv(a("b6", 0, 256), "Er0", every("GA", 512, 4608))
        tt(a("yv"), a("b4"), a("hiT"), SUB)
        cp(ind(a("WK"), u(10)), a("yv"))
        mm(a("b7", 0, 256), a("ID"), a("tie"), True, False)
        conv(a("b7", 0, 256), "Ek", every("WK", 512, 4608), False, True)
        tt(a("lv", 256, 512), a("lvI", 0, 256), a("lv", 0, 256), ADD)
        tt(a("lv", 768, 1024), a("lv", 512, 768), med("drow"), MUL)
        tt(a("lv", 256, 512), a("lv", 256, 512), a("lv", 768, 1024), ADD)
        tt(a("b6", 256, 512), a("b6", 0, 256), med("x613"), MUL)
        tt(a("lvI", 256, 512), a("b6", 256, 512), a("lv", 256, 512), ADD)
        ts(a("lvI", 256, 512), a("lvI", 256, 512), 4095, AND)
        tt(a("lv", 768, 1024), a("lvI", 256, 512), a("on16"), ADD)
        cp(a("offM"), a("lv", 768, 1024))
        for ch in range(4):
            act(a("GL", 1024 * ch, 1024 * ch + 1024), ind(a("W"), a("offM", 64 * ch, 64 * ch + 64)))

        def level_scan(ch):
            lo = 1024 * ch
            scan(a("sc", lo, lo + 1024), a("mask"), a("GL", lo, lo + 1024), 0.0, MAX)

        if t == 0:
            consts_d()
            for ch in range(4):
                kmax_key("kp", None, ch)
            later[1] = kmax_fin("b1", 224, "km1")
        if t == 1:
            gather_n("V", 4)
            for ch in (5, 6, 7):
                gather_n("S", ch)
            kmax_key("b5", "C0", 0)
            kmax_pe("b5", 1)
        if t:
            later[3]()
        cp(a("tk", 64, 192), a("b7", 128, 256))
        tt(a("tk", 192, 320), a("b7", 0, 128), a("tk", 64, 192), MAX)
        tt(a("tk", 320, 384), a("tk", 192, 256), a("tk", 256, 320), MAX)
        tt(a("tk", 384, 416), a("tk", 320, 352), a("tk", 352, 384), MAX)
        tt(a("kwI", 0, 16), a("tk", 384, 400), a("tk", 400, 416), MAX)
        ts(a("kwI", 16, 32), a("kwI", 0, 16), 3840, AND)
        tt(a("sB", 0, 16), a("cB"), a("kwI", 16, 32), SUB)
        cp(a("sU", 480, 496), a("sB", 0, 16))
        cp(a("wr"), ind(a("WK", 512, 4608), a("sU", 480, 496)))
        tt(a("sB", 16, 32), a("kwI", 0, 16), a("thK"), GT)
        cp(a("sBb", 0, 16), a("sB", 16, 32))
        conv(a("b1", 128, 144), "Eo", every("wr", 0, 256))
        mm(a("b4", 0, 256), a("BDo2"), a("wr"), True, True)
        if t < 2:
            mm(a("b3", 128, 144), a("ones", 0, 128), a("sBb", 0, 16), True, True)
        level_scan(0)
        tt(a("sB", 32, 48), a("b1", 128, 144), a("sB", 16, 32), MUL)
        ts(a("sBb", 16, 32), a("sB", 32, 48), 512.5, GT)
        mm(a("b2", 128, 144), a("BD"), a("sBb", 16, 32), True, True)
        mm(a("b2", 144, 160), a("TRI"), a("sBb", 16, 32), True, True)
        tt(a("eqo"), med("LSp"), a("b4", 0, 256), EQ)
        mm(a("b1", 192, 208), a("ID"), a("full"), True, False)
        conv(a("b1", 192, 208), "E1", every("eqo", 0, 256), False, True)
        ts(a("sB", 48, 64), a("sB", 32, 48), -512.0, ADD, 0.0, MAX)
        scan(a("sB", 64, 80), a("ones", 0, 16), a("b2", 128, 144), -60.0, ADD)
        tt(a("sB", 80, 96), a("sB", 64, 80), a("b2", 144, 160), LE)
        tt(a("sB", 96, 112), a("sB", 80, 96), a("sB", 48, 64), MUL)
        ts(a("kwI", 0, 16), a("sB", 96, 112), -1.0, ADD)
        ts(a("kwI", 16, 32), a("kwI", 0, 16), 15, AND)
        ts(a("kwI", 0, 16), a("kwI", 0, 16), 4, SHR)
        cp(a("sB", 112, 144), a("kwI", 0, 32))
        tt(a("rt"), ind(a("sB", 112, 128), a("offR")), a("x32"), EQ)
        for h in range(16):
            ts(a("lt", 128 * h, 128 * h + 128), a("Tlo"), a("sB", 128 + h, 129 + h), EQ)
            mm(a("b2", 192, 224), a("lt", 128 * h, 128 * h + 128), a("rt", 32 * h, 32 * h + 32), h == 0, h == 15)
        ts(a("sB", 144, 160), a("sB", 32, 48), 512.5, LT)
        cp(a("hs%d" % t), a("b2", 192, 224))
        send(up, "hs%d" % t, "hl%d" % t, 32, "ah%d" % t, "lh%d" % t)
        tt(a("sB", 144, 160), a("sB", 144, 160), a("b1", 192, 208), GT)
        tt(a("jv"), a("sB", 144, 160), a("sB", 32, 48), MUL)
        cp(a("jw", 0, 16), a("jv"))
        tt(a("jw", 16, 32), a("jv"), a("jw", 0, 16), SUB)
        if t == 0:
            consts_e()
        if t < 2:
            for h in range(2):
                k = 128 * (2 * par + h)
                mm(a("b3", 160 + h, 192, 2), a("HX", k, k + 128), a("jv"), True, True)

        def jv_rows():
            rows("b2", a("jw", 0, 16), 16, 256, a("jw", 16, 32))

        if t == 2:
            jv_rows()
        if t == 1:
            kmax_key("b5", "C0", 1)
            kmax_pe("b5", 2)
        level_scan(1)
        if t == 0:
            ts(a("jw", 32, 48), a("jv"), 1.0, MIN)
            rows("b2", a("jw", 32, 48), 16, 256)
            act(a("sg"), a("b2", 256, 512))
        if t < 2:
            if t == 0:
                cp(a("oX"), a("b3", 160, 192))
            else:
                tt(a("oX"), a("oX"), a("b3", 160, 192), ADD)
            cp(u(14), a("oX"))
            act(a("gr"), ind(a("T01", 0, 513), u(14)))
            tt(f(30), a("oX"), a("c15m"), ADD)
            tt(i(13), a("gl%d" % (t + 1)), a("hs%d" % t), ADD)
            ts(i(14), i(13), 15, AND)
            cp(a("rowh", 32, 64), i(14))
        level_scan(2)
        level_scan(3)
        mm(a("b6", 256, 512), a("ID"), a(zt, 0, 256), True, False)
        mm(a("b6", 256, 512), a("ID"), a("sc", 15, 4096, 16), False, True)
        if t == 1:
            kmax_key("b5", "C0", 2)
            kmax_pe("b5", 3)
        act(a("zf"), a("b6", 256, 512), 0.5, -0.25)
        act(a("zf"), a("zf"), 1.0, 12582912.0)
        act(a("zs"), a("zf"), 1.0, -12582912.0)
        send((rank + 1 + t) % N, "zs", "z%d" % (t + 1), 256, "az%d" % t, "lz%d" % t)

        def lists(t=t, med=med):
            tt(a("lv", 1024, 1280), a("b2", 256, 512), a("mk", 256 * (t & 1), 256 * (t & 1) + 256), MUL)
            tt(med("LSp"), med("LSp"), a("lv", 1024, 1280), ADD)
            if t == 0:
                tt(a("nrow", 0, 512, 2), a("nrow", 0, 512, 2), a("sg"), ADD)

        def limits():
            emit("V", a("sB", 160, 161), [a("b3", 128, 144)], lambda e: e.tensor_reduce(a("sB", 160, 161)[0], a("b3", 128, 144)[0], axis=AxisListType.X, op=ADD))
            cp(a("kwI", 0, 1), a("sB", 160, 161))
            ts(a("kwI", 1, 2), a("kwI", 0, 1), 31, AND)
            cp(a("sB", 161, 162), a("kwI", 1, 2))
            ts(a("thT"), a("thB"), a("sB", 161, 162), ADD, 4080.0, MIN)
            ts(a("thK"), a("thT"), 4096.0, MUL, 4095.0, ADD)

        if t < 2:
            conv(a("b3", 192, 224), "En1" if t == 0 else "En0", every("gr", 0, 512))
            iota(a("WK", 512), [[0, 4096]], 0, 0)
        tt(i(13), f(25), a("hl%d" % t), ADD)
        ts(i(14), i(13), 15, AND)
        cp(a("rowh", 0, 32), i(14))
        rows("b4", a("rowh", 0, 32), 32)
        if t == 0:
            tt(a("T01", 1, 513, 2), a("T01", 1, 513, 2), a("sg"), ADD)
            gather_n("S", 0)
        elif t == 1:
            kmax_key("b5", "C0", 3)
            later[1] = kmax_fin("b1", 224, "km2")
        if t < 2:
            tt(f(31), f(30), a("b3", 192, 224), ADD)
            later[1]()
            act(a("drow", 0, 512), a("b4"))
            cp(a("dA"), i(14))
            trial_tables()
            later[0], later[2], later[3] = limits, jv_rows, lists
        else:
            lists()
            ts(a("ky"), a("LSp", 0, 512), -1.0, ADD)
            dma("D", T.yl[:, :], a("ky")[0], [(("ky", 0, 512), False)])
            act(a("kyT"), a("b4"))
            dma("D", T.yd[:, :], T.kyT[0:128:16, :], [(("kyT", 0, 512), False)])
            dma("D", T.yz[:, :], T.z3[:, :], [(("z3", 0, 256), False)])
    for s, v in total.items():
        g.wait_ge(T.sem[s], v)
